import numpy as np
import ml_dtypes


def mxq(x, axis, fmt="e4m3"):
    dtype, down = {"e4m3": (ml_dtypes.float8_e4m3fn, 7), "e5m2": (ml_dtypes.float8_e5m2, 14)}[fmt]
    v = np.moveaxis(np.asarray(x, np.float32).astype(ml_dtypes.bfloat16).astype(np.float64), axis, -1)
    blocks = v.reshape(v.shape[:-1] + (-1, 32))
    amax = np.abs(blocks).max(-1, keepdims=True)
    byte = np.maximum(np.where(amax > 0, np.frexp(amax)[1] - 1 + 127, 0) - down, 1)
    scale = np.exp2(byte - 127.0)
    codes = (blocks / scale).astype(np.float32).astype(dtype).astype(np.float64)
    return np.moveaxis((codes * scale).reshape(v.shape), -1, axis)


WIDE = False


def mx_kscale(k):
    if not WIDE:
        return np.ones(k)
    levels = np.array([10, -10, 5, -5, 0])
    if k % 512:
        return np.exp2(np.random.permutation(np.resize(levels, k // 32))).repeat(32)
    a = np.empty((k // 512, 16))
    for p in range(k // 512):
        a[p, :8] = np.random.permutation(np.resize(levels, 8))
        for g in range(8):
            far = levels[np.abs(levels - a[p, g]) >= 10]
            a[p, g + 8] = far[np.random.randint(len(far))]
    return np.exp2(a.ravel()).repeat(32)


def f64(x):
    return np.asarray(x).astype(np.float64)


def striped(idx):
    return np.tile(idx.reshape(-1, 16).T, (8, 1)).astype(np.uint16)


def unstriped(offs):
    return offs[:16].T.reshape(-1).astype(np.int64)


E2M1 = np.array([0.0, 0.5, 1.0, 1.5, 2.0, 3.0, 4.0, 6.0, -0.0, -0.5, -1.0, -1.5, -2.0, -3.0, -4.0, -6.0])


def pack_weight(w, fmt):
    k, n = w.shape
    w = f64(np.asarray(w, np.float32).astype(ml_dtypes.bfloat16)).reshape(k // 32, 32, n)
    amax = np.abs(w).max(1)
    if fmt == "e4m3":
        byte = np.frexp(amax)[1] - 1 + 127 - 7
    else:
        mant, ex = np.frexp(amax / 6.0)
        byte = np.where(mant > 0.5, ex, ex - 1) + 127
    byte = np.clip(np.where(amax > 0, byte, 1), 1, 254)
    scaled = (w * np.exp2(127.0 - byte)[:, None, :]).reshape(k, n).astype(np.float32)
    by_word = np.ascontiguousarray(scaled.reshape(k // 512, 128, 4, n).transpose(0, 1, 3, 2))
    if fmt == "e4m3":
        words = by_word.astype(ml_dtypes.float8_e4m3fn).view(np.uint8)
    else:
        c = by_word.astype(ml_dtypes.float4_e2m1fn).view(np.uint8) & 0xF
        words = (c[..., 0::2] | (c[..., 1::2] << 4)).reshape(k // 512, 128, 2 * n)
    return np.ascontiguousarray(words), np.ascontiguousarray(byte.astype(np.uint8).reshape(k // 512, 16, n))


def unpack_weight(words, scales, fmt):
    g, _, n = scales.shape
    words = np.ascontiguousarray(words).reshape(g, 128, n, -1)
    if fmt == "e4m3":
        vals = words.view(ml_dtypes.float8_e4m3fn).astype(np.float64)
    else:
        nib = np.empty((g, 128, n, 4), np.uint8)
        nib[..., 0::2] = words & 0xF
        nib[..., 1::2] = words >> 4
        vals = E2M1[nib]
    vals = vals * np.repeat(np.exp2(scales.astype(np.float64) - 127.0), 8, axis=1)[..., None]
    return vals.transpose(0, 1, 3, 2).reshape(g * 512, n)


def gelu(v):
    return 0.5 * v * (1.0 + np.tanh(np.sqrt(2.0 / np.pi) * (v + 0.044715 * v**3)))


def bf(x):
    return np.asarray(x, np.float32).astype(ml_dtypes.bfloat16)


def planes(Y):
    n, m = Y.shape
    b = f64(bf(Y)).reshape(n // 32, 32, m)
    amax = np.abs(b).max(1)
    byte = np.clip(np.where(amax > 0, np.frexp(amax)[1] - 1 + 127 - 7, 1), 1, 254)
    codes = (b * np.exp2(127.0 - byte)[:, None, :]).reshape(n, m).astype(np.float32).astype(ml_dtypes.float8_e4m3fn).view(np.uint8)
    words = codes.reshape(n // 512, 128, 4, m).transpose(0, 1, 3, 2)
    return np.ascontiguousarray(words), np.ascontiguousarray(byte.astype(np.uint8).reshape(n // 512, 16, m))


K, H, N, T, S = 1024, 1024, 512, 2048, 1024

def setup_inputs():
    n = np.random.standard_normal
    s = mx_kscale(K)[:, None]
    u = mx_kscale(H)[:, None]
    size = np.exp(0.8 * n(N))
    tab_words, tab_scales = pack_weight(n((K, T)) * s, "e4m3")
    w4_words, w4_scales = pack_weight(2.0 * n((H, N)) / np.sqrt(H) / u, "e2m1")
    return {
        "tab_words": tab_words,
        "tab_scales": tab_scales,
        "offs": striped(np.random.permutation(T)[:S]),
        "gT": (n((N, T)) * size[:, None]).astype(np.float32),
        "w1": (n((K, H)) / np.sqrt(K) / s * u.T).astype(np.float32),
        "b1": (0.5 * n(H) * u[:, 0]).astype(np.float32),
        "w2": (1.5 * n((H, N)) / np.sqrt(H) / u * size[None, :]).astype(np.float32),
        "w4_words": w4_words,
        "w4_scales": w4_scales,
    }

def reference(tab_words, tab_scales, offs, gT, w1, b1, w2, w4_words, w4_scales):
    v = unpack_weight(tab_words, tab_scales, "e4m3")[:, unstriped(offs)]
    h = mxq(f64(w1), 0, "e4m3").T @ v
    h = np.maximum(h + f64(b1)[:, None], 0.0)
    hq = mxq(h, 0, "e4m3")
    a = mxq(f64(w2), 0, "e4m3").T @ hq
    b = unpack_weight(w4_words, w4_scales, "e2m1").T @ hq
    gate = 1.0 / (1.0 + np.exp(-b))
    g = f64(gT)[:, unstriped(offs)]
    new = g + a * gate
    y = f64(gT).copy()
    y[:, unstriped(offs)] = new
    words, scales = planes(y)
    return y, words, scales

@@ -1,0 +1,376 @@
+from contextlib import ExitStack
+
+import concourse.mybir as mybir
+
+K, H, N, T, S = 1024, 1024, 512, 2048, 1024
+FLOPS = 2 * K * H * S + 2 * 2 * H * N * S
+
+F32 = mybir.dt.float32
+BF16 = mybir.dt.bfloat16
+I32 = mybir.dt.int32
+U32 = mybir.dt.uint32
+U16 = mybir.dt.uint16
+U8 = mybir.dt.uint8
+FP8X4 = mybir.dt.float8_e4m3fn_x4
+FP4X4 = mybir.dt.float4_e2m1fn_x4
+ACT = mybir.ActivationFunctionType
+ALU = mybir.AluOpType
+
+P = 128
+PACK = 4
+W = 512
+HALVES = S // W
+PASSES = 2
+CHUNKS = T // W
+
+
+def tile_list_stroke_correction_kernel(
+    tc, tab_words, tab_scales, offs, gT, w1, b1, w2, w4_words, w4_scales, out_0, out_1, out_2
+):
+    nc = tc.nc
+
+    def copy_on(engine, out, in_):
+        if engine == "S":
+            nc.scalar.copy(out, in_)
+        elif engine == "G":
+            nc.gpsimd.tensor_scalar(out, in_, 1.0, 0.0, ALU.mult, ALU.add)
+        else:
+            nc.vector.tensor_copy(out, in_)
+
+    with ExitStack() as ctx:
+        keep = ctx.enter_context(tc.tile_pool(name="keep", bufs=1))
+        ring = ctx.enter_context(tc.tile_pool(name="ring", bufs=3))
+        psum_h = ctx.enter_context(tc.psum_pool(name="psum_h", bufs=4))
+        psum_o = ctx.enter_context(tc.psum_pool(name="psum_o", bufs=2))
+
+        offsets = keep.tile([P, S // 16], U16, name="offsets")
+        nc.sync.dma_start(offsets[:], offs)
+
+        def listed(tile_ap, half):
+            return tile_ap.indirect(offsets[:, half * (W // 16) : (half + 1) * (W // 16)])
+
+        tab_plane = keep.tile([P, T // 4], I32, name="tab_plane", align_bytes=64)
+        w4_plane_raw = keep.tile([P, PASSES * N // 4], I32, name="w4_plane_raw", align_bytes=64)
+        nc.vector.memset(tab_plane[:], 0)
+        nc.vector.memset(w4_plane_raw[:], 0)
+        warm = keep.tile([P, 1], F32, name="warm")
+        nc.vector.memset(warm[:], 0.0)
+        warm_out = keep.tile([P, 1], F32, name="warm_out")
+        nc.scalar.activation(warm_out[:], warm[:], ACT.Sigmoid)
+
+        def clock(ap, dtype, name):
+            tick = keep.tile([P, 1], dtype, name=name)
+            nc.gpsimd.tensor_copy(tick[:], ap)
+
+        raw = {}
+        tab_raw = {}
+        page = {}
+        bias = keep.tile([P, PASSES, PACK], F32, name="bias")
+        w4_raw = keep.tile([P, PASSES * 2 * N // 4], I32, name="w4_raw", align_bytes=64)
+
+        def load_w(name, src, a, b):
+            raw[name, a, b] = keep.tile([P, PACK, W], F32, name=f"raw_{name}_{a}_{b}", tag=f"raw_{name}_{a}_{b}", align_bytes=64)
+            rows = src[a * W : (a + 1) * W, b * W : (b + 1) * W]
+            nc.sync.dma_start(raw[name, a, b][:], rows.rearrange("(p j) c -> p j c", j=PACK))
+
+        def load_tab(a):
+            tab_raw[a] = keep.tile([P, T], I32, name=f"tab_raw_{a}")
+            nc.sync.dma_start(tab_raw[a][:], tab_words[a].rearrange("p n i -> p (n i)").bitcast(I32))
+
+        def load_tab_plane():
+            for q in range(4):
+                nc.scalar.dma_start(tab_plane[32 * q : 32 * q + 8, :], tab_scales[:, 4 * q : 4 * q + 4, :].bitcast(I32))
+
+        def load_w4():
+            nc.scalar.dma_start(
+                w4_raw[:].rearrange("p (a c) -> p a c", a=PASSES), w4_words.bitcast(I32).rearrange("a p c -> p a c")
+            )
+
+        def load_w4_plane():
+            for q in range(4):
+                nc.scalar.dma_start(
+                    w4_plane_raw[32 * q : 32 * q + 4, :].rearrange("p (a c) -> p a c", a=PASSES),
+                    w4_scales[:, 4 * q : 4 * q + 4, :].bitcast(I32).rearrange("a r c -> r a c"),
+                )
+
+        def load_bias():
+            nc.scalar.dma_start(bias[:], b1.rearrange("(b p t) -> p b t", b=PASSES, t=PACK))
+
+        def load_page(t):
+            page[t] = keep.tile([P, T], F32, name=f"page_{t}")
+            nc.sync.dma_start(page[t][:], gT.rearrange("(p t) m -> t p m", t=PACK)[t])
+
+        load_w4()
+        load_tab_plane()
+        load_w4_plane()
+        load_bias()
+        load_w("w1", w1, 0, 0)
+        load_tab(0)
+        load_w("w1", w1, 1, 0)
+        load_tab(1)
+        load_w("w1", w1, 0, 1)
+        load_w("w1", w1, 1, 1)
+        load_w("w2", w2, 0, 0)
+        load_page(0)
+        load_w("w2", w2, 1, 0)
+        load_page(1)
+        load_page(2)
+        load_page(3)
+
+        codes = {}
+        planes = {}
+
+        def quantise(key, grouped_ap, cols):
+            name = "_".join(str(k) for k in key)
+            codes[key] = keep.tile([P, cols], U32, name=f"codes_{name}", align_bytes=64)
+            planes[key] = keep.tile([P, cols], U8, name=f"plane_{name}", align_bytes=64)
+            nc.vector.quantize_mx(out=codes[key][:].bitcast(FP8X4), scales=planes[key][:], in_=grouped_ap)
+
+        def prepare_w(name, a, b, engine):
+            grouped = ring.tile([P, PACK * W], BF16, name="grouped", align_bytes=64)
+            copy_on(
+                engine,
+                grouped[:].rearrange("p (t m j) -> p m j t", t=PACK, j=PACK),
+                raw[name, a, b][:].rearrange("p j (m t) -> p m j t", t=PACK),
+            )
+            quantise((name, a, b), grouped[:], W)
+
+        v_codes = {}
+        v_plane = {}
+
+        def gather_words(a, half):
+            v_codes[a, half] = keep.tile([P, W], U32, name=f"v_codes_{a}_{half}", align_bytes=64)
+            nc.vector.tensor_copy(v_codes[a, half][:], listed(tab_raw[a][:].bitcast(U32), half))
+
+        def gather_plane(half):
+            v_plane[half] = keep.tile([P, W], U8, name=f"v_plane_{half}", align_bytes=64)
+            nc.vector.tensor_copy(v_plane[half][:], listed(tab_plane[:].bitcast(U8), half))
+
+        w4_codes = keep.tile([P, PASSES * 2 * N], U8, name="w4_codes", align_bytes=64)
+        w4_plane = keep.tile([P, PASSES * N], U8, name="w4_plane", align_bytes=64)
+
+        def prepare_w4():
+            nc.vector.tensor_copy(
+                w4_codes[:].rearrange("p (a t m y) -> p a t m y", a=PASSES, t=PACK, y=2),
+                w4_raw[:].bitcast(U8).rearrange("p (a m t y) -> p a t m y", a=PASSES, t=PACK, y=2),
+            )
+
+        def prepare_w4_plane():
+            nc.vector.tensor_copy(
+                w4_plane[:].rearrange("p (a t m) -> p a t m", a=PASSES, t=PACK),
+                w4_plane_raw[:].bitcast(U8).rearrange("p (a m t) -> p a t m", a=PASSES, t=PACK),
+            )
+
+        def interleave(engine, rows_tile):
+            grouped = ring.tile([P, PACK * W], BF16, name="grouped", align_bytes=64)
+            copy_on(
+                engine,
+                grouped[:].rearrange("p (c i t) -> p c t i", i=4, t=PACK),
+                rows_tile.rearrange("p t (c i) -> p c t i", i=4),
+            )
+            return grouped
+
+        banks = [psum_h.tile([P, W], F32, name=f"h_bank_{t}", bufs=1) for t in range(PACK)]
+        h_rows = {}
+
+        def hidden(half, b, reuse=None):
+            for a in range(PASSES):
+                for t in range(PACK):
+                    cols = slice(t * P, (t + 1) * P)
+                    nc.tensor.matmul_mx(
+                        out=banks[t][:],
+                        lhsT=codes["w1", a, b][:, cols].bitcast(FP8X4),
+                        lhsT_scale=planes["w1", a, b][:, cols],
+                        rhs=v_codes[a, half][:].bitcast(FP8X4),
+                        rhs_scale=v_plane[half][4 * a : P, :],
+                        start=(a == 0),
+                        stop=(a == PASSES - 1),
+                    )
+            if reuse is None:
+                h_rows[half, b] = keep.tile([P, PACK, W], BF16, name=f"h_rows_{half}_{b}", tag=f"h_rows_{half}_{b}", align_bytes=64)[:]
+            else:
+                spent = raw[reuse][:].rearrange("p j c -> p (j c)").bitcast(BF16)
+                h_rows[half, b] = spent[:, 0 : PACK * W].rearrange("p (t c) -> p t c", t=PACK)
+            for t in range(PACK):
+                nc.scalar.activation(h_rows[half, b][:, t, :], banks[t][:], ACT.Relu, bias=bias[:, b, t : t + 1])
+
+        def quantise_hidden(half, b, engine):
+            quantise(("h", half, b), interleave(engine, h_rows[half, b])[:], W)
+
+        state = {}
+
+        def gather_state(t, half):
+            state[t, half] = keep.tile([P, W], F32, name=f"state_{t}_{half}")[:]
+            nc.vector.tensor_copy(state[t, half], listed(page[t][:], half))
+
+        def gather_state_whole(t, reuse=None):
+            if reuse is None:
+                whole = keep.tile([P, S], F32, name=f"state_{t}")[:]
+            else:
+                whole = h_rows[reuse].rearrange("p t c -> p (t c)").bitcast(F32)
+            nc.vector.tensor_copy(whole, page[t][:].indirect(offsets[:]))
+            for half in range(HALVES):
+                state[t, half] = whole[:, half * W : (half + 1) * W]
+
+        gate = {}
+        a_banks = [psum_o.tile([P, W], F32, name=f"a_bank_{i}", bufs=1) for i in range(2)]
+        b_banks = [psum_o.tile([P, W], F32, name=f"b_bank_{i}", bufs=1) for i in range(2)]
+
+        def make_gate(t, half, onto=None):
+            bank = b_banks[len(gate) % 2]
+            for a in range(PASSES):
+                nc.tensor.matmul_mx(
+                    out=bank[:],
+                    lhsT=w4_codes[:, 2 * (a * N + t * P) : 2 * (a * N + (t + 1) * P)].bitcast(FP4X4),
+                    lhsT_scale=w4_plane[:, a * N + t * P : a * N + (t + 1) * P],
+                    rhs=codes["h", half, a][:].bitcast(FP8X4),
+                    rhs_scale=planes["h", half, a][:],
+                    start=(a == 0),
+                    stop=(a == PASSES - 1),
+                )
+            if onto is None:
+                gate[t, half] = keep.tile([P, W], F32, name=f"gate_{t}_{half}")[:]
+            else:
+                gate[t, half] = onto.rearrange("p t c -> p (t c)").bitcast(F32)[:, 0:W]
+            nc.scalar.activation(gate[t, half], bank[:], ACT.Sigmoid)
+
+        step = {}
+        step_ring = [keep.tile([P, W], F32, name=f"step_{i}") for i in range(3)]
+
+        def make_step(t, half):
+            bank = a_banks[len(step) % 2]
+            cols = slice(t * P, (t + 1) * P)
+            for a in range(PASSES):
+                nc.tensor.matmul_mx(
+                    out=bank[:],
+                    lhsT=codes["w2", a, 0][:, cols].bitcast(FP8X4),
+                    lhsT_scale=planes["w2", a, 0][:, cols],
+                    rhs=codes["h", half, a][:].bitcast(FP8X4),
+                    rhs_scale=planes["h", half, a][:],
+                    start=(a == 0),
+                    stop=(a == PASSES - 1),
+                )
+            step[t, half] = step_ring[len(step) % 3]
+            nc.vector.tensor_tensor(step[t, half][:], bank[:], gate[t, half], ALU.mult)
+
+        def scatter(t, half):
+            nc.vector.tensor_tensor(listed(page[t][:], half), state[t, half], step[t, half][:], ALU.add)
+
+        y_rows = [keep.tile([P, PACK, W], BF16, name=f"y_rows_{c}") for c in range(CHUNKS)]
+        y_plane = keep.tile([P, T], U8, name="y_plane", align_bytes=64)
+
+        def store_page(t):
+            nc.sync.dma_start(out_0.rearrange("(p t) m -> t p m", t=PACK)[t], page[t][:])
+
+        def round_page(t, c, engine):
+            copy_on(engine, y_rows[c][:, t, :], page[t][:, c * W : (c + 1) * W])
+
+        def finish_chunk(c, engine):
+            grouped = interleave(engine, y_rows[c][:])
+            y_codes = ring.tile([P, W], I32, name="y_codes", align_bytes=64)
+            nc.vector.quantize_mx(
+                out=y_codes[:].bitcast(FP8X4), scales=y_plane[:, c * W : (c + 1) * W], in_=grouped[:]
+            )
+            nc.sync.dma_start(
+                out_1[0].rearrange("p m i -> p (m i)")[:, c * W * PACK : (c + 1) * W * PACK].bitcast(I32), y_codes[:]
+            )
+
+        y_grouped = [keep.tile([P, W, PACK], BF16, name=f"y_grouped_{c}", tag=f"raw_w1_{c % 2}_{c // 2}", align_bytes=64) for c in range(CHUNKS)]
+
+        def weave_pair(c, u, engine):
+            copy_on(
+                engine,
+                y_grouped[c][:, :, 2 * u : 2 * u + 2].rearrange("p (c i) t -> p c t i", i=4),
+                y_rows[c][:, 2 * u : 2 * u + 2, :].rearrange("p t (c i) -> p c t i", i=4),
+            )
+
+        def quantise_chunk(c):
+            y_codes = keep.tile([P, W], I32, name=f"y_codes_{c}", align_bytes=64)
+            nc.vector.quantize_mx(
+                out=y_codes[:].bitcast(FP8X4),
+                scales=y_plane[:, c * W : (c + 1) * W],
+                in_=y_grouped[c][:].rearrange("p c t -> p (c t)"),
+            )
+            nc.sync.dma_start(
+                out_1[0].rearrange("p m i -> p (m i)")[:, c * W * PACK : (c + 1) * W * PACK].bitcast(I32), y_codes[:]
+            )
+
+        def store_plane():
+            for q in range(4):
+                (nc.scalar if q % 2 else nc.sync).dma_start(
+                    out_2[0, 4 * q : 4 * q + 4, :].bitcast(I32), y_plane[32 * q : 32 * q + 4, :].bitcast(I32)
+                )
+
+        prepare_w4()
+        gather_plane(0)
+        prepare_w("w1", 0, 0, "S")
+        gather_words(0, 0)
+        prepare_w("w1", 1, 0, "S")
+        gather_words(1, 0)
+        hidden(0, 0)
+        prepare_w("w1", 0, 1, "V")
+        prepare_w("w1", 1, 1, "V")
+        hidden(0, 1)
+        quantise_hidden(0, 0, "S")
+        quantise_hidden(0, 1, "S")
+        prepare_w("w2", 0, 0, "S")
+        prepare_w("w2", 1, 0, "S")
+        prepare_w4_plane()
+        make_gate(0, 0)
+        gather_state_whole(0)
+        make_step(0, 0)
+        gather_words(0, 1)
+        gather_plane(1)
+        gather_words(1, 1)
+        scatter(0, 0)
+        make_gate(1, 0)
+        hidden(1, 0, ("w2", 1, 0))
+        make_gate(2, 0)
+        quantise_hidden(1, 0, "S")
+        hidden(1, 1, None)
+        quantise_hidden(1, 1, "S")
+        make_gate(0, 1)
+        make_gate(1, 1)
+        make_gate(2, 1)
+        make_gate(3, 0)
+        make_gate(3, 1)
+        gather_state_whole(1)
+        gather_state_whole(2)
+        gather_state_whole(3, (1, 1))
+        make_step(1, 0)
+        scatter(1, 0)
+        make_step(2, 0)
+        scatter(2, 0)
+        make_step(0, 1)
+        scatter(0, 1)
+        store_page(0)
+        for c in range(CHUNKS):
+            round_page(0, c, "S")
+        make_step(1, 1)
+        scatter(1, 1)
+        store_page(1)
+        for c in range(CHUNKS):
+            round_page(1, c, "S")
+        for c in range(CHUNKS):
+            weave_pair(c, 0, "S")
+        make_step(2, 1)
+        scatter(2, 1)
+        store_page(2)
+        for c in range(CHUNKS):
+            round_page(2, c, "S")
+        make_step(3, 0)
+        scatter(3, 0)
+        make_step(3, 1)
+        scatter(3, 1)
+        store_page(3)
+        round_page(3, 0, "V")
+        round_page(3, 2, "S")
+        round_page(3, 1, "V")
+        weave_pair(0, 1, "V")
+        weave_pair(2, 1, "S")
+        round_page(3, 3, "S")
+        weave_pair(1, 1, "V")
+        weave_pair(3, 1, "S")
+        for c in (0, 1, 2, 3):
+            quantise_chunk(c)
+        store_plane()

@@ -18,125 +18,115 @@ ALU = mybir.AluOpType
 
 P = 128
 PACK = 4
-W = 512
-HALVES = S // W
+W = P * PACK
 PASSES = 2
+QUADS = 4
+PER_COLUMN = 16
 CHUNKS = T // W
+VECTOR_CHUNKS, SCALAR_CHUNKS = (0, 1), (2, 3)
+RUN = 4
 
 
 def tile_list_stroke_correction_kernel(
     tc, tab_words, tab_scales, offs, gT, w1, b1, w2, w4_words, w4_scales, out_0, out_1, out_2
 ):
     nc = tc.nc
-
-    def copy_on(engine, out, in_):
-        if engine == "S":
-            nc.scalar.copy(out, in_)
-        elif engine == "G":
-            nc.gpsimd.tensor_scalar(out, in_, 1.0, 0.0, ALU.mult, ALU.add)
-        else:
-            nc.vector.tensor_copy(out, in_)
+    on_scalar, on_vector = nc.scalar.copy, nc.vector.tensor_copy
 
     with ExitStack() as ctx:
         keep = ctx.enter_context(tc.tile_pool(name="keep", bufs=1))
-        ring = ctx.enter_context(tc.tile_pool(name="ring", bufs=3))
-        psum_h = ctx.enter_context(tc.psum_pool(name="psum_h", bufs=4))
-        psum_o = ctx.enter_context(tc.psum_pool(name="psum_o", bufs=2))
+        psum = ctx.enter_context(tc.psum_pool(name="psum", bufs=1))
 
-        offsets = keep.tile([P, S // 16], U16, name="offsets")
+        offsets = keep.tile([P, S // PER_COLUMN], U16, name="offsets")
         nc.sync.dma_start(offsets[:], offs)
 
-        def listed(tile_ap, half):
-            return tile_ap.indirect(offsets[:, half * (W // 16) : (half + 1) * (W // 16)])
+        def listed(window, half):
+            columns = W // PER_COLUMN
+            return window.indirect(offsets[:, half * columns : (half + 1) * columns])
 
         tab_plane = keep.tile([P, T // 4], I32, name="tab_plane", align_bytes=64)
         w4_plane_raw = keep.tile([P, PASSES * N // 4], I32, name="w4_plane_raw", align_bytes=64)
         nc.vector.memset(tab_plane[:], 0)
         nc.vector.memset(w4_plane_raw[:], 0)
-        warm = keep.tile([P, 1], F32, name="warm")
-        nc.vector.memset(warm[:], 0.0)
-        warm_out = keep.tile([P, 1], F32, name="warm_out")
-        nc.scalar.activation(warm_out[:], warm[:], ACT.Sigmoid)
 
-        def clock(ap, dtype, name):
-            tick = keep.tile([P, 1], dtype, name=name)
-            nc.gpsimd.tensor_copy(tick[:], ap)
-
-        raw = {}
-        tab_raw = {}
-        page = {}
         bias = keep.tile([P, PASSES, PACK], F32, name="bias")
+        nc.scalar.dma_start(bias[:], b1.rearrange("(b p t) -> p b t", b=PASSES, t=PACK))
         w4_raw = keep.tile([P, PASSES * 2 * N // 4], I32, name="w4_raw", align_bytes=64)
+        nc.sync.dma_start(
+            w4_raw[:].rearrange("p (a c) -> p a c", a=PASSES), w4_words.bitcast(I32).rearrange("a p c -> p a c")
+        )
+        for q in range(QUADS):
+            nc.scalar.dma_start(tab_plane[32 * q : 32 * q + 8, :], tab_scales[:, 4 * q : 4 * q + 4, :].bitcast(I32))
+        for q in range(QUADS):
+            nc.scalar.dma_start(
+                w4_plane_raw[32 * q : 32 * q + 4, :].rearrange("p (a c) -> p a c", a=PASSES),
+                w4_scales[:, 4 * q : 4 * q + 4, :].bitcast(I32).rearrange("a r c -> r a c"),
+            )
 
-        def load_w(name, src, a, b):
-            raw[name, a, b] = keep.tile([P, PACK, W], F32, name=f"raw_{name}_{a}_{b}", tag=f"raw_{name}_{a}_{b}", align_bytes=64)
+        raw, tab_raw, page = {}, {}, {}
+
+        def load_weight(name, src, a, b):
+            tag = f"raw_{name}_{a}_{b}"
+            raw[name, a, b] = keep.tile([P, PACK, W], F32, name=tag, tag=tag, align_bytes=64)
             rows = src[a * W : (a + 1) * W, b * W : (b + 1) * W]
             nc.sync.dma_start(raw[name, a, b][:], rows.rearrange("(p j) c -> p j c", j=PACK))
 
-        def load_tab(a):
+        def load_table(a):
             tab_raw[a] = keep.tile([P, T], I32, name=f"tab_raw_{a}")
             nc.sync.dma_start(tab_raw[a][:], tab_words[a].rearrange("p n i -> p (n i)").bitcast(I32))
-
-        def load_tab_plane():
-            for q in range(4):
-                nc.scalar.dma_start(tab_plane[32 * q : 32 * q + 8, :], tab_scales[:, 4 * q : 4 * q + 4, :].bitcast(I32))
-
-        def load_w4():
-            nc.scalar.dma_start(
-                w4_raw[:].rearrange("p (a c) -> p a c", a=PASSES), w4_words.bitcast(I32).rearrange("a p c -> p a c")
-            )
-
-        def load_w4_plane():
-            for q in range(4):
-                nc.scalar.dma_start(
-                    w4_plane_raw[32 * q : 32 * q + 4, :].rearrange("p (a c) -> p a c", a=PASSES),
-                    w4_scales[:, 4 * q : 4 * q + 4, :].bitcast(I32).rearrange("a r c -> r a c"),
-                )
-
-        def load_bias():
-            nc.scalar.dma_start(bias[:], b1.rearrange("(b p t) -> p b t", b=PASSES, t=PACK))
 
         def load_page(t):
             page[t] = keep.tile([P, T], F32, name=f"page_{t}")
             nc.sync.dma_start(page[t][:], gT.rearrange("(p t) m -> t p m", t=PACK)[t])
 
-        load_w4()
-        load_tab_plane()
-        load_w4_plane()
-        load_bias()
-        load_w("w1", w1, 0, 0)
-        load_tab(0)
-        load_w("w1", w1, 1, 0)
-        load_tab(1)
-        load_w("w1", w1, 0, 1)
-        load_w("w1", w1, 1, 1)
-        load_w("w2", w2, 0, 0)
+        for a in range(PASSES):
+            load_weight("w1", w1, a, 0)
+        for a in range(PASSES):
+            load_table(a)
+        for a in range(PASSES):
+            load_weight("w1", w1, a, 1)
         load_page(0)
-        load_w("w2", w2, 1, 0)
         load_page(1)
+        for a in range(PASSES):
+            load_weight("w2", w2, a, 0)
         load_page(2)
         load_page(3)
 
-        codes = {}
-        planes = {}
+        warm_out = keep.tile([P, 1], F32, name="warm_out")
+        nc.scalar.activation(warm_out[:], bias[:, 0, 0:1], ACT.Sigmoid)
 
-        def quantise(key, grouped_ap, cols):
-            name = "_".join(str(k) for k in key)
-            codes[key] = keep.tile([P, cols], U32, name=f"codes_{name}", align_bytes=64)
-            planes[key] = keep.tile([P, cols], U8, name=f"plane_{name}", align_bytes=64)
-            nc.vector.quantize_mx(out=codes[key][:].bitcast(FP8X4), scales=planes[key][:], in_=grouped_ap)
+        staging = [keep.tile([P, PACK * W], BF16, name=f"staging_{i}", align_bytes=64) for i in range(4)]
+        codes, planes = {}, {}
+        shared_plane = keep.tile([P, W], U8, name="shared_plane", align_bytes=64)
+        planes["w1", 1, 1] = shared_plane[4:P, :]
+        planes["h", 0, 0] = shared_plane[:]
 
-        def prepare_w(name, a, b, engine):
-            grouped = ring.tile([P, PACK * W], BF16, name="grouped", align_bytes=64)
-            copy_on(
-                engine,
-                grouped[:].rearrange("p (t m j) -> p m j t", t=PACK, j=PACK),
+        def quantise(key, woven):
+            name = "_".join(str(part) for part in key)
+            codes[key] = keep.tile([P, W], U32, name=f"codes_{name}", align_bytes=64)
+            if key not in planes:
+                planes[key] = keep.tile([P, W], U8, name=f"plane_{name}", align_bytes=64)[:]
+            nc.vector.quantize_mx(out=codes[key][:].bitcast(FP8X4), scales=planes[key], in_=woven[:])
+
+        def prepare_weight(name, a, b, copy, woven):
+            copy(
+                woven[:].rearrange("p (t m j) -> p m j t", t=PACK, j=PACK),
                 raw[name, a, b][:].rearrange("p j (m t) -> p m j t", t=PACK),
             )
-            quantise((name, a, b), grouped[:], W)
+            quantise((name, a, b), woven)
 
-        v_codes = {}
-        v_plane = {}
+        w4_codes = keep.tile([P, PASSES * 2 * N], U8, name="w4_codes", align_bytes=64)
+        w4_plane = keep.tile([P, PASSES * N], U8, name="w4_plane", align_bytes=64)
+        nc.vector.tensor_copy(
+            w4_codes[:].bitcast(U16).rearrange("p (a t m) -> p a t m", a=PASSES, t=PACK),
+            w4_raw[:].bitcast(U16).rearrange("p (a m t) -> p a t m", a=PASSES, t=PACK),
+        )
+        nc.vector.tensor_copy(
+            w4_plane[:].rearrange("p (a t m) -> p a t m", a=PASSES, t=PACK),
+            w4_plane_raw[:].bitcast(U8).rearrange("p (a m t) -> p a t m", a=PASSES, t=PACK),
+        )
+
+        v_codes, v_plane = {}, {}
 
         def gather_words(a, half):
             v_codes[a, half] = keep.tile([P, W], U32, name=f"v_codes_{a}_{half}", align_bytes=64)
@@ -146,39 +136,18 @@ def tile_list_stroke_correction_kernel(
             v_plane[half] = keep.tile([P, W], U8, name=f"v_plane_{half}", align_bytes=64)
             nc.vector.tensor_copy(v_plane[half][:], listed(tab_plane[:].bitcast(U8), half))
 
-        w4_codes = keep.tile([P, PASSES * 2 * N], U8, name="w4_codes", align_bytes=64)
-        w4_plane = keep.tile([P, PASSES * N], U8, name="w4_plane", align_bytes=64)
+        h_banks = [psum.tile([P, W], F32, name=f"h_bank_{t}") for t in range(PACK)]
+        a_banks = [psum.tile([P, W], F32, name=f"a_bank_{i}") for i in range(2)]
+        b_banks = [psum.tile([P, W], F32, name=f"b_bank_{i}") for i in range(2)]
+        h_rows = {key: keep.tile([P, PACK, W], BF16, name=f"h_rows_{key[0]}_{key[1]}", align_bytes=64)[:]
+                  for key in ((0, 0), (0, 1), (1, 1))}
 
-        def prepare_w4():
-            nc.vector.tensor_copy(
-                w4_codes[:].rearrange("p (a t m y) -> p a t m y", a=PASSES, t=PACK, y=2),
-                w4_raw[:].bitcast(U8).rearrange("p (a m t y) -> p a t m y", a=PASSES, t=PACK, y=2),
-            )
-
-        def prepare_w4_plane():
-            nc.vector.tensor_copy(
-                w4_plane[:].rearrange("p (a t m) -> p a t m", a=PASSES, t=PACK),
-                w4_plane_raw[:].bitcast(U8).rearrange("p (a m t) -> p a t m", a=PASSES, t=PACK),
-            )
-
-        def interleave(engine, rows_tile):
-            grouped = ring.tile([P, PACK * W], BF16, name="grouped", align_bytes=64)
-            copy_on(
-                engine,
-                grouped[:].rearrange("p (c i t) -> p c t i", i=4, t=PACK),
-                rows_tile.rearrange("p t (c i) -> p c t i", i=4),
-            )
-            return grouped
-
-        banks = [psum_h.tile([P, W], F32, name=f"h_bank_{t}", bufs=1) for t in range(PACK)]
-        h_rows = {}
-
-        def hidden(half, b, reuse=None):
+        def hidden(half, b):
             for a in range(PASSES):
                 for t in range(PACK):
                     cols = slice(t * P, (t + 1) * P)
                     nc.tensor.matmul_mx(
-                        out=banks[t][:],
+                        out=h_banks[t][:],
                         lhsT=codes["w1", a, b][:, cols].bitcast(FP8X4),
                         lhsT_scale=planes["w1", a, b][:, cols],
                         rhs=v_codes[a, half][:].bitcast(FP8X4),
@@ -186,191 +155,148 @@ def tile_list_stroke_correction_kernel(
                         start=(a == 0),
                         stop=(a == PASSES - 1),
                     )
-            if reuse is None:
-                h_rows[half, b] = keep.tile([P, PACK, W], BF16, name=f"h_rows_{half}_{b}", tag=f"h_rows_{half}_{b}", align_bytes=64)[:]
-            else:
-                spent = raw[reuse][:].rearrange("p j c -> p (j c)").bitcast(BF16)
-                h_rows[half, b] = spent[:, 0 : PACK * W].rearrange("p (t c) -> p t c", t=PACK)
             for t in range(PACK):
-                nc.scalar.activation(h_rows[half, b][:, t, :], banks[t][:], ACT.Relu, bias=bias[:, b, t : t + 1])
+                nc.scalar.activation(h_rows[half, b][:, t, :], h_banks[t][:], ACT.Relu, bias=bias[:, b, t : t + 1])
 
-        def quantise_hidden(half, b, engine):
-            quantise(("h", half, b), interleave(engine, h_rows[half, b])[:], W)
+        def quantise_hidden(half, b, woven):
+            nc.scalar.copy(
+                woven[:].rearrange("p (c i t) -> p c t i", i=RUN, t=PACK),
+                h_rows[half, b].rearrange("p t (c i) -> p c t i", i=RUN),
+            )
+            quantise(("h", half, b), woven)
 
-        state = {}
+        state, gate, step = {}, {}, {}
+        step_ring = [keep.tile([P, W], F32, name=f"step_{i}") for i in range(4)]
 
-        def gather_state(t, half):
-            state[t, half] = keep.tile([P, W], F32, name=f"state_{t}_{half}")[:]
-            nc.vector.tensor_copy(state[t, half], listed(page[t][:], half))
+        def gather_state(t, picked):
+            nc.vector.tensor_copy(picked, page[t][:].indirect(offsets[:]))
+            for half in range(S // W):
+                state[t, half] = picked[:, half * W : (half + 1) * W]
 
-        def gather_state_whole(t, reuse=None):
-            if reuse is None:
-                whole = keep.tile([P, S], F32, name=f"state_{t}")[:]
-            else:
-                whole = h_rows[reuse].rearrange("p t c -> p (t c)").bitcast(F32)
-            nc.vector.tensor_copy(whole, page[t][:].indirect(offsets[:]))
-            for half in range(HALVES):
-                state[t, half] = whole[:, half * W : (half + 1) * W]
-
-        gate = {}
-        a_banks = [psum_o.tile([P, W], F32, name=f"a_bank_{i}", bufs=1) for i in range(2)]
-        b_banks = [psum_o.tile([P, W], F32, name=f"b_bank_{i}", bufs=1) for i in range(2)]
-
-        def make_gate(t, half, onto=None):
-            bank = b_banks[len(gate) % 2]
+        def second_product(bank, half, weight):
             for a in range(PASSES):
+                lhsT, lhsT_scale = weight(a)
                 nc.tensor.matmul_mx(
                     out=bank[:],
-                    lhsT=w4_codes[:, 2 * (a * N + t * P) : 2 * (a * N + (t + 1) * P)].bitcast(FP4X4),
-                    lhsT_scale=w4_plane[:, a * N + t * P : a * N + (t + 1) * P],
+                    lhsT=lhsT,
+                    lhsT_scale=lhsT_scale,
                     rhs=codes["h", half, a][:].bitcast(FP8X4),
-                    rhs_scale=planes["h", half, a][:],
+                    rhs_scale=planes["h", half, a],
                     start=(a == 0),
                     stop=(a == PASSES - 1),
                 )
-            if onto is None:
-                gate[t, half] = keep.tile([P, W], F32, name=f"gate_{t}_{half}")[:]
-            else:
-                gate[t, half] = onto.rearrange("p t c -> p (t c)").bitcast(F32)[:, 0:W]
-            nc.scalar.activation(gate[t, half], bank[:], ACT.Sigmoid)
 
-        step = {}
-        step_ring = [keep.tile([P, W], F32, name=f"step_{i}") for i in range(3)]
+        def make_gate(t, half, bank, into):
+            def w4_slice(a):
+                first = a * N + t * P
+                return w4_codes[:, 2 * first : 2 * (first + P)].bitcast(FP4X4), w4_plane[:, first : first + P]
 
-        def make_step(t, half):
-            bank = a_banks[len(step) % 2]
+            second_product(bank, half, w4_slice)
+            gate[t, half] = into
+            nc.scalar.activation(into, bank[:], ACT.Sigmoid)
+
+        def make_step(t, half, bank, into):
             cols = slice(t * P, (t + 1) * P)
-            for a in range(PASSES):
-                nc.tensor.matmul_mx(
-                    out=bank[:],
-                    lhsT=codes["w2", a, 0][:, cols].bitcast(FP8X4),
-                    lhsT_scale=planes["w2", a, 0][:, cols],
-                    rhs=codes["h", half, a][:].bitcast(FP8X4),
-                    rhs_scale=planes["h", half, a][:],
-                    start=(a == 0),
-                    stop=(a == PASSES - 1),
-                )
-            step[t, half] = step_ring[len(step) % 3]
-            nc.vector.tensor_tensor(step[t, half][:], bank[:], gate[t, half], ALU.mult)
+            second_product(bank, half, lambda a: (codes["w2", a, 0][:, cols].bitcast(FP8X4), planes["w2", a, 0][:, cols]))
+            step[t, half] = into
+            nc.vector.tensor_tensor(into, bank[:], gate[t, half], ALU.mult)
 
         def scatter(t, half):
-            nc.vector.tensor_tensor(listed(page[t][:], half), state[t, half], step[t, half][:], ALU.add)
+            nc.vector.tensor_tensor(listed(page[t][:], half), state[t, half], step[t, half], ALU.add)
 
-        y_rows = [keep.tile([P, PACK, W], BF16, name=f"y_rows_{c}") for c in range(CHUNKS)]
-        y_plane = keep.tile([P, T], U8, name="y_plane", align_bytes=64)
+        def as_float32(rows):
+            return rows.rearrange("p t c -> p (t c)").bitcast(F32)
 
-        def store_page(t):
-            nc.sync.dma_start(out_0.rearrange("(p t) m -> t p m", t=PACK)[t], page[t][:])
-
-        def round_page(t, c, engine):
-            copy_on(engine, y_rows[c][:, t, :], page[t][:, c * W : (c + 1) * W])
-
-        def finish_chunk(c, engine):
-            grouped = interleave(engine, y_rows[c][:])
-            y_codes = ring.tile([P, W], I32, name="y_codes", align_bytes=64)
-            nc.vector.quantize_mx(
-                out=y_codes[:].bitcast(FP8X4), scales=y_plane[:, c * W : (c + 1) * W], in_=grouped[:]
-            )
-            nc.sync.dma_start(
-                out_1[0].rearrange("p m i -> p (m i)")[:, c * W * PACK : (c + 1) * W * PACK].bitcast(I32), y_codes[:]
-            )
-
-        y_grouped = [keep.tile([P, W, PACK], BF16, name=f"y_grouped_{c}", tag=f"raw_w1_{c % 2}_{c // 2}", align_bytes=64) for c in range(CHUNKS)]
-
-        def weave_pair(c, u, engine):
-            copy_on(
-                engine,
-                y_grouped[c][:, :, 2 * u : 2 * u + 2].rearrange("p (c i) t -> p c t i", i=4),
-                y_rows[c][:, 2 * u : 2 * u + 2, :].rearrange("p t (c i) -> p c t i", i=4),
-            )
-
-        def quantise_chunk(c):
-            y_codes = keep.tile([P, W], I32, name=f"y_codes_{c}", align_bytes=64)
-            nc.vector.quantize_mx(
-                out=y_codes[:].bitcast(FP8X4),
-                scales=y_plane[:, c * W : (c + 1) * W],
-                in_=y_grouped[c][:].rearrange("p c t -> p (c t)"),
-            )
-            nc.sync.dma_start(
-                out_1[0].rearrange("p m i -> p (m i)")[:, c * W * PACK : (c + 1) * W * PACK].bitcast(I32), y_codes[:]
-            )
-
-        def store_plane():
-            for q in range(4):
-                (nc.scalar if q % 2 else nc.sync).dma_start(
-                    out_2[0, 4 * q : 4 * q + 4, :].bitcast(I32), y_plane[32 * q : 32 * q + 4, :].bitcast(I32)
-                )
-
-        prepare_w4()
-        gather_plane(0)
-        prepare_w("w1", 0, 0, "S")
         gather_words(0, 0)
-        prepare_w("w1", 1, 0, "S")
+        gather_plane(0)
+        prepare_weight("w1", 0, 0, on_scalar, staging[0])
+        prepare_weight("w1", 1, 0, on_scalar, staging[1])
         gather_words(1, 0)
         hidden(0, 0)
-        prepare_w("w1", 0, 1, "V")
-        prepare_w("w1", 1, 1, "V")
+        prepare_weight("w1", 0, 1, on_vector, staging[2])
+        prepare_weight("w1", 1, 1, on_vector, staging[3])
         hidden(0, 1)
-        quantise_hidden(0, 0, "S")
-        quantise_hidden(0, 1, "S")
-        prepare_w("w2", 0, 0, "S")
-        prepare_w("w2", 1, 0, "S")
-        prepare_w4_plane()
-        make_gate(0, 0)
-        gather_state_whole(0)
-        make_step(0, 0)
+        quantise_hidden(0, 0, staging[0])
+        quantise_hidden(0, 1, staging[1])
+        prepare_weight("w2", 0, 0, on_vector, staging[2])
+        prepare_weight("w2", 1, 0, on_scalar, staging[3])
         gather_words(0, 1)
         gather_plane(1)
         gather_words(1, 1)
+
+        spent = raw["w2", 1, 0]
+        make_gate(0, 0, b_banks[0], spent[:, 2, :])
+        make_gate(1, 0, b_banks[1], spent[:, 3, :])
+        for t in range(PACK - 1):
+            gather_state(t, keep.tile([P, S], F32, name=f"state_{t}")[:])
+        make_step(0, 0, a_banks[0], step_ring[0][:])
+        make_step(1, 0, a_banks[1], step_ring[1][:])
+        h_rows[1, 0] = spent[:, 0:2, :].rearrange("p j c -> p (j c)").bitcast(BF16).rearrange("p (t c) -> p t c", t=PACK)
+        hidden(1, 0)
+        quantise_hidden(1, 0, staging[0])
+        make_gate(2, 0, b_banks[0], as_float32(h_rows[1, 0])[:, 0:W])
+        hidden(1, 1)
+        quantise_hidden(1, 1, staging[1])
+        last_state = as_float32(h_rows[1, 1])
+        gather_state(PACK - 1, last_state)
         scatter(0, 0)
-        make_gate(1, 0)
-        hidden(1, 0, ("w2", 1, 0))
-        make_gate(2, 0)
-        quantise_hidden(1, 0, "S")
-        hidden(1, 1, None)
-        quantise_hidden(1, 1, "S")
-        make_gate(0, 1)
-        make_gate(1, 1)
-        make_gate(2, 1)
-        make_gate(3, 0)
-        make_gate(3, 1)
-        gather_state_whole(1)
-        gather_state_whole(2)
-        gather_state_whole(3, (1, 1))
-        make_step(1, 0)
         scatter(1, 0)
-        make_step(2, 0)
+        make_step(2, 0, a_banks[0], step_ring[2][:])
         scatter(2, 0)
-        make_step(0, 1)
-        scatter(0, 1)
-        store_page(0)
+
+        late = [(0, 1), (1, 1), (2, 1), (3, 0), (3, 1)]
+        last_steps = keep.tile([P, S], F32, name="last_steps")
+        late_b_banks = [b_banks[1], b_banks[0], h_banks[0], h_banks[1], h_banks[2]]
+        late_a_banks = [a_banks[1], h_banks[3], a_banks[0]]
+        for i, (t, half) in enumerate(late):
+            make_gate(t, half, late_b_banks[i], keep.tile([P, W], F32, name=f"gate_{t}_{half}")[:])
+            into = last_steps[:, half * W : (half + 1) * W] if t == PACK - 1 else step_ring[len(step) % len(step_ring)][:]
+            make_step(t, half, late_a_banks[i % len(late_a_banks)], into)
+            if t > 0 and half == 1:
+                scatter(t - 1, 1)
+        nc.vector.tensor_tensor(page[PACK - 1][:].indirect(offsets[:]), last_state, last_steps[:], ALU.add)
+        for t in range(PACK):
+            nc.sync.dma_start(out_0.rearrange("(p t) m -> t p m", t=PACK)[t], page[t][:])
+
+        y_rows = keep.tile([P, PACK, T], BF16, name="y_rows")
+        y_woven = [
+            keep.tile([P, W, PACK], BF16, name=f"y_woven_{c}", tag=f"raw_w1_{c % 2}_{c // 2}", align_bytes=64)
+            for c in range(CHUNKS)
+        ]
+        y_plane = keep.tile([P, T], U8, name="y_plane", align_bytes=64)
+
+        def chunk(c):
+            return slice(c * W, (c + 1) * W)
+
+        def weave(c, first, last, copy):
+            copy(
+                y_woven[c][:, :, first:last].rearrange("p (c i) t -> p c t i", i=RUN),
+                y_rows[:, first:last, chunk(c)].rearrange("p t (c i) -> p c t i", i=RUN),
+            )
+
+        front, back = slice(0, T // 2), slice(T // 2, T)
+        for t in range(PACK - 1):
+            for cols in (front, back) if t < 2 else (back, front):
+                nc.scalar.copy(y_rows[:, t, cols], page[t][:, cols])
+            if t == 1:
+                for c in VECTOR_CHUNKS:
+                    weave(c, 0, 2, on_scalar)
+        for c in SCALAR_CHUNKS:
+            weave(c, 0, 3, on_scalar)
+        for c in SCALAR_CHUNKS:
+            nc.scalar.copy(y_woven[c][:, :, 3], page[3][:, chunk(c)])
+        for c in VECTOR_CHUNKS:
+            nc.vector.tensor_copy(y_rows[:, 3, chunk(c)], page[3][:, chunk(c)])
+        for c in VECTOR_CHUNKS:
+            weave(c, 2, 4, on_vector)
+
+        out_words = out_1[0].rearrange("p m i -> p (m i)").bitcast(I32)
         for c in range(CHUNKS):
-            round_page(0, c, "S")
-        make_step(1, 1)
-        scatter(1, 1)
-        store_page(1)
-        for c in range(CHUNKS):
-            round_page(1, c, "S")
-        for c in range(CHUNKS):
-            weave_pair(c, 0, "S")
-        make_step(2, 1)
-        scatter(2, 1)
-        store_page(2)
-        for c in range(CHUNKS):
-            round_page(2, c, "S")
-        make_step(3, 0)
-        scatter(3, 0)
-        make_step(3, 1)
-        scatter(3, 1)
-        store_page(3)
-        round_page(3, 0, "V")
-        round_page(3, 2, "S")
-        round_page(3, 1, "V")
-        weave_pair(0, 1, "V")
-        weave_pair(2, 1, "S")
-        round_page(3, 3, "S")
-        weave_pair(1, 1, "V")
-        weave_pair(3, 1, "S")
-        for c in (0, 1, 2, 3):
-            quantise_chunk(c)
-        store_plane()
+            y_codes = keep.tile([P, W], I32, name=f"y_codes_{c}", align_bytes=64)
+            nc.vector.quantize_mx(
+                out=y_codes[:].bitcast(FP8X4), scales=y_plane[:, chunk(c)], in_=y_woven[c][:].rearrange("p m t -> p (m t)")
+            )
+            nc.sync.dma_start(out_words[:, chunk(c)], y_codes[:])
+        for q in range(QUADS):
+            queue = nc.scalar if q % 2 else nc.sync
+            queue.dma_start(out_2[0, 4 * q : 4 * q + 4, :].bitcast(I32), y_plane[32 * q : 32 * q + 4, :].bitcast(I32))

@@ -79,16 +79,16 @@ def tile_list_stroke_correction_kernel(
             page[t] = keep.tile([P, T], F32, name=f"page_{t}")
             nc.sync.dma_start(page[t][:], gT.rearrange("(p t) m -> t p m", t=PACK)[t])
 
-        for a in range(PASSES):
-            load_weight("w1", w1, a, 0)
-        for a in range(PASSES):
-            load_table(a)
-        for a in range(PASSES):
-            load_weight("w1", w1, a, 1)
+        load_table(0)
+        load_weight("w1", w1, 0, 0)
+        load_weight("w1", w1, 1, 0)
+        load_table(1)
+        load_weight("w1", w1, 0, 1)
+        load_weight("w1", w1, 1, 1)
         load_page(0)
         load_page(1)
-        for a in range(PASSES):
-            load_weight("w2", w2, a, 0)
+        load_weight("w2", w2, 0, 0)
+        load_weight("w2", w2, 1, 0)
         load_page(2)
         load_page(3)
 
@@ -258,45 +258,45 @@ def tile_list_stroke_correction_kernel(
         for t in range(PACK):
             nc.sync.dma_start(out_0.rearrange("(p t) m -> t p m", t=PACK)[t], page[t][:])
 
-        y_rows = keep.tile([P, PACK, T], BF16, name="y_rows")
+        y_rows = [keep.tile([P, PACK, W], BF16, name=f"y_rows_{c}") for c in range(CHUNKS)]
         y_woven = [
             keep.tile([P, W, PACK], BF16, name=f"y_woven_{c}", tag=f"raw_w1_{c % 2}_{c // 2}", align_bytes=64)
             for c in range(CHUNKS)
         ]
         y_plane = keep.tile([P, T], U8, name="y_plane", align_bytes=64)
 
-        def chunk(c):
-            return slice(c * W, (c + 1) * W)
+        def chunk_of_page(t, c):
+            return page[t][:, c * W : (c + 1) * W]
 
         def weave(c, first, last, copy):
             copy(
                 y_woven[c][:, :, first:last].rearrange("p (c i) t -> p c t i", i=RUN),
-                y_rows[:, first:last, chunk(c)].rearrange("p t (c i) -> p c t i", i=RUN),
+                y_rows[c][:, first:last, :].rearrange("p t (c i) -> p c t i", i=RUN),
             )
 
-        front, back = slice(0, T // 2), slice(T // 2, T)
         for t in range(PACK - 1):
-            for cols in (front, back) if t < 2 else (back, front):
-                nc.scalar.copy(y_rows[:, t, cols], page[t][:, cols])
+            for c in range(CHUNKS):
+                nc.scalar.copy(y_rows[c][:, t, :], chunk_of_page(t, c))
             if t == 1:
                 for c in VECTOR_CHUNKS:
                     weave(c, 0, 2, on_scalar)
         for c in SCALAR_CHUNKS:
             weave(c, 0, 3, on_scalar)
         for c in SCALAR_CHUNKS:
-            nc.scalar.copy(y_woven[c][:, :, 3], page[3][:, chunk(c)])
+            nc.scalar.copy(y_woven[c][:, :, 3], chunk_of_page(3, c))
         for c in VECTOR_CHUNKS:
-            nc.vector.tensor_copy(y_rows[:, 3, chunk(c)], page[3][:, chunk(c)])
+            nc.vector.tensor_copy(y_rows[c][:, 3, :], chunk_of_page(3, c))
         for c in VECTOR_CHUNKS:
             weave(c, 2, 4, on_vector)
 
         out_words = out_1[0].rearrange("p m i -> p (m i)").bitcast(I32)
         for c in range(CHUNKS):
+            cols = slice(c * W, (c + 1) * W)
             y_codes = keep.tile([P, W], I32, name=f"y_codes_{c}", align_bytes=64)
             nc.vector.quantize_mx(
-                out=y_codes[:].bitcast(FP8X4), scales=y_plane[:, chunk(c)], in_=y_woven[c][:].rearrange("p m t -> p (m t)")
+                out=y_codes[:].bitcast(FP8X4), scales=y_plane[:, cols], in_=y_woven[c][:].rearrange("p m t -> p (m t)")
             )
-            nc.sync.dma_start(out_words[:, chunk(c)], y_codes[:])
+            nc.sync.dma_start(out_words[:, cols], y_codes[:])
         for q in range(QUADS):
             queue = nc.scalar if q % 2 else nc.sync
             queue.dma_start(out_2[0, 4 * q : 4 * q + 4, :].bitcast(I32), y_plane[32 * q : 32 * q + 4, :].bitcast(I32))

@@ -23,8 +23,9 @@ PASSES = 2
 QUADS = 4
 PER_COLUMN = 16
 CHUNKS = T // W
-VECTOR_CHUNKS, SCALAR_CHUNKS = (0, 1), (2, 3)
 RUN = 4
+KIB = 1024
+UNITS = ((0, 0), (1, 0), (0, 1), (1, 1), (2, 0), (2, 1), (3, 0), (3, 1))
 
 
 def tile_list_stroke_correction_kernel(
@@ -35,14 +36,17 @@ def tile_list_stroke_correction_kernel(
 
     with ExitStack() as ctx:
         keep = ctx.enter_context(tc.tile_pool(name="keep", bufs=1))
+        shared = ctx.enter_context(tc.tile_pool(name="shared", bufs=1))
         psum = ctx.enter_context(tc.psum_pool(name="psum", bufs=1))
+
+        def placed(name, shape, dtype, kib):
+            return shared.tile(shape, dtype, name=name, align_bytes=64, offset=int(kib * KIB))
 
         offsets = keep.tile([P, S // PER_COLUMN], U16, name="offsets")
         nc.sync.dma_start(offsets[:], offs)
 
-        def listed(window, half):
-            columns = W // PER_COLUMN
-            return window.indirect(offsets[:, half * columns : (half + 1) * columns])
+        def listed(window, lo, hi):
+            return window.indirect(offsets[:, lo // PER_COLUMN : hi // PER_COLUMN])
 
         tab_plane = keep.tile([P, T // 4], I32, name="tab_plane", align_bytes=64)
         w4_plane_raw = keep.tile([P, PASSES * N // 4], I32, name="w4_plane_raw", align_bytes=64)
@@ -64,10 +68,10 @@ def tile_list_stroke_correction_kernel(
             )
 
         raw, tab_raw, page = {}, {}, {}
+        raw_place = {("w1", 0, 0): 0, ("w1", 1, 0): 8, ("w1", 0, 1): 16, ("w1", 1, 1): 24, ("w2", 0, 0): 32, ("w2", 1, 0): 40}
 
         def load_weight(name, src, a, b):
-            tag = f"raw_{name}_{a}_{b}"
-            raw[name, a, b] = keep.tile([P, PACK, W], F32, name=tag, tag=tag, align_bytes=64)
+            raw[name, a, b] = placed(f"raw_{name}_{a}_{b}", [P, PACK, W], F32, raw_place[name, a, b])
             rows = src[a * W : (a + 1) * W, b * W : (b + 1) * W]
             nc.sync.dma_start(raw[name, a, b][:], rows.rearrange("(p j) c -> p j c", j=PACK))
 
@@ -86,92 +90,92 @@ def tile_list_stroke_correction_kernel(
         load_weight("w1", w1, 0, 1)
         load_weight("w1", w1, 1, 1)
         load_page(0)
-        load_page(1)
         load_weight("w2", w2, 0, 0)
         load_weight("w2", w2, 1, 0)
-        load_page(2)
-        load_page(3)
+        for t in range(1, PACK):
+            load_page(t)
 
         warm_out = keep.tile([P, 1], F32, name="warm_out")
         nc.scalar.activation(warm_out[:], bias[:, 0, 0:1], ACT.Sigmoid)
 
-        staging = [keep.tile([P, PACK * W], BF16, name=f"staging_{i}", align_bytes=64) for i in range(4)]
-        codes, planes = {}, {}
-        shared_plane = keep.tile([P, W], U8, name="shared_plane", align_bytes=64)
-        planes["w1", 1, 1] = shared_plane[4:P, :]
-        planes["h", 0, 0] = shared_plane[:]
+        staging = [keep.tile([P, PACK * W], BF16, name=f"staging_{i}", align_bytes=64) for i in range(2)]
+        staging_once = placed("staging_once", [P, PACK * W], BF16, 61)
+        w_codes, w_plane = {}, {}
 
-        def quantise(key, woven):
-            name = "_".join(str(part) for part in key)
-            codes[key] = keep.tile([P, W], U32, name=f"codes_{name}", align_bytes=64)
-            if key not in planes:
-                planes[key] = keep.tile([P, W], U8, name=f"plane_{name}", align_bytes=64)[:]
-            nc.vector.quantize_mx(out=codes[key][:].bitcast(FP8X4), scales=planes[key], in_=woven[:])
+        def round_weight(name, a, b, woven, on_scalar_to):
+            key = name, a, b
+            out = woven[:].rearrange("p (t m j) -> p m j t", t=PACK, j=PACK)
+            src = raw[key][:].rearrange("p j (m t) -> p m j t", t=PACK)
+            if on_scalar_to > 0:
+                on_scalar(out[:, :on_scalar_to], src[:, :on_scalar_to])
+            if on_scalar_to < P:
+                on_vector(out[:, on_scalar_to:], src[:, on_scalar_to:])
 
-        def prepare_weight(name, a, b, copy, woven):
-            copy(
-                woven[:].rearrange("p (t m j) -> p m j t", t=PACK, j=PACK),
-                raw[name, a, b][:].rearrange("p j (m t) -> p m j t", t=PACK),
-            )
-            quantise((name, a, b), woven)
+        def prepare_weight(name, a, b, woven, on_scalar_to):
+            round_weight(name, a, b, woven, on_scalar_to)
+            quantise_weight(name, a, b, woven)
+
+        def quantise_weight(name, a, b, woven):
+            key = name, a, b
+            if name == "w2":
+                w_codes[key] = placed(f"codes_w2_{a}", [P, W], U32, 16 + 4 * a)
+            else:
+                w_codes[key] = keep.tile([P, W], U32, name=f"codes_{name}_{a}_{b}", align_bytes=64)
+            w_plane[key] = keep.tile([P, W], U8, name=f"plane_{name}_{a}_{b}", align_bytes=64)
+            nc.vector.quantize_mx(out=w_codes[key][:].bitcast(FP8X4), scales=w_plane[key][:], in_=woven[:])
 
         w4_codes = keep.tile([P, PASSES * 2 * N], U8, name="w4_codes", align_bytes=64)
-        w4_plane = keep.tile([P, PASSES * N], U8, name="w4_plane", align_bytes=64)
         nc.vector.tensor_copy(
             w4_codes[:].bitcast(U16).rearrange("p (a t m) -> p a t m", a=PASSES, t=PACK),
             w4_raw[:].bitcast(U16).rearrange("p (a m t) -> p a t m", a=PASSES, t=PACK),
         )
-        nc.vector.tensor_copy(
-            w4_plane[:].rearrange("p (a t m) -> p a t m", a=PASSES, t=PACK),
-            w4_plane_raw[:].bitcast(U8).rearrange("p (a m t) -> p a t m", a=PASSES, t=PACK),
-        )
 
-        v_codes, v_plane = {}, {}
+        v_codes = [keep.tile([P, S], U32, name=f"v_codes_{a}", align_bytes=64) for a in range(PASSES)]
+        v_plane = keep.tile([P, S], U8, name="v_plane", align_bytes=64)
 
         def gather_words(a, half):
-            v_codes[a, half] = keep.tile([P, W], U32, name=f"v_codes_{a}_{half}", align_bytes=64)
-            nc.vector.tensor_copy(v_codes[a, half][:], listed(tab_raw[a][:].bitcast(U32), half))
+            lo, hi = half * W, (half + 1) * W
+            nc.vector.tensor_copy(v_codes[a][:, lo:hi], listed(tab_raw[a][:].bitcast(U32), lo, hi))
 
         def gather_plane(half):
-            v_plane[half] = keep.tile([P, W], U8, name=f"v_plane_{half}", align_bytes=64)
-            nc.vector.tensor_copy(v_plane[half][:], listed(tab_plane[:].bitcast(U8), half))
+            lo, hi = half * W, (half + 1) * W
+            nc.vector.tensor_copy(v_plane[:, lo:hi], listed(tab_plane[:].bitcast(U8), lo, hi))
 
-        h_banks = [psum.tile([P, W], F32, name=f"h_bank_{t}") for t in range(PACK)]
-        a_banks = [psum.tile([P, W], F32, name=f"a_bank_{i}") for i in range(2)]
-        b_banks = [psum.tile([P, W], F32, name=f"b_bank_{i}") for i in range(2)]
-        h_rows = {key: keep.tile([P, PACK, W], BF16, name=f"h_rows_{key[0]}_{key[1]}", align_bytes=64)[:]
-                  for key in ((0, 0), (0, 1), (1, 1))}
+        banks = [psum.tile([P, W], F32, name=f"bank_{i}") for i in range(2 * PACK)]
 
-        def hidden(half, b):
+        def hidden(half, b, rows):
+            sums = banks[half * PACK : (half + 1) * PACK]
+            entries = slice(half * W, (half + 1) * W)
             for a in range(PASSES):
                 for t in range(PACK):
                     cols = slice(t * P, (t + 1) * P)
                     nc.tensor.matmul_mx(
-                        out=h_banks[t][:],
-                        lhsT=codes["w1", a, b][:, cols].bitcast(FP8X4),
-                        lhsT_scale=planes["w1", a, b][:, cols],
-                        rhs=v_codes[a, half][:].bitcast(FP8X4),
-                        rhs_scale=v_plane[half][4 * a : P, :],
+                        out=sums[t][:],
+                        lhsT=w_codes["w1", a, b][:, cols].bitcast(FP8X4),
+                        lhsT_scale=w_plane["w1", a, b][:, cols],
+                        rhs=v_codes[a][:, entries].bitcast(FP8X4),
+                        rhs_scale=v_plane[4 * a : P, entries],
                         start=(a == 0),
                         stop=(a == PASSES - 1),
                     )
             for t in range(PACK):
-                nc.scalar.activation(h_rows[half, b][:, t, :], h_banks[t][:], ACT.Relu, bias=bias[:, b, t : t + 1])
+                nc.scalar.activation(rows[:, t, :], sums[t][:], ACT.Relu, bias=bias[:, b, t : t + 1])
 
-        def quantise_hidden(half, b, woven):
+        def weave_on_scalar(woven, rows):
             nc.scalar.copy(
                 woven[:].rearrange("p (c i t) -> p c t i", i=RUN, t=PACK),
-                h_rows[half, b].rearrange("p t (c i) -> p c t i", i=RUN),
+                rows[:].rearrange("p t (c i) -> p c t i", i=RUN),
             )
-            quantise(("h", half, b), woven)
 
-        state, gate, step = {}, {}, {}
-        step_ring = [keep.tile([P, W], F32, name=f"step_{i}") for i in range(4)]
+        def weave_on_gpsimd(woven, rows):
+            nc.gpsimd.tensor_copy(woven[:].rearrange("p (c t) -> p c t", t=PACK), rows[:].rearrange("p t c -> p c t"))
 
-        def gather_state(t, picked):
-            nc.vector.tensor_copy(picked, page[t][:].indirect(offsets[:]))
-            for half in range(S // W):
-                state[t, half] = picked[:, half * W : (half + 1) * W]
+        h_codes, h_plane = {}, {}
+
+        def quantise_hidden(half, b, woven):
+            h_codes[half, b] = keep.tile([P, W], U32, name=f"h_codes_{half}_{b}", align_bytes=64)
+            h_plane[half, b] = keep.tile([P, W], U8, name=f"h_plane_{half}_{b}", align_bytes=64)
+            nc.vector.quantize_mx(out=h_codes[half, b][:].bitcast(FP8X4), scales=h_plane[half, b][:], in_=woven[:])
 
         def second_product(bank, half, weight):
             for a in range(PASSES):
@@ -180,114 +184,143 @@ def tile_list_stroke_correction_kernel(
                     out=bank[:],
                     lhsT=lhsT,
                     lhsT_scale=lhsT_scale,
-                    rhs=codes["h", half, a][:].bitcast(FP8X4),
-                    rhs_scale=planes["h", half, a],
+                    rhs=h_codes[half, a][:].bitcast(FP8X4),
+                    rhs_scale=h_plane[half, a][:],
                     start=(a == 0),
                     stop=(a == PASSES - 1),
                 )
 
-        def make_gate(t, half, bank, into):
+        state = {}
+
+        def gather_state(t):
+            state[t] = keep.tile([P, S], F32, name=f"state_{t}")
+            nc.vector.tensor_copy(state[t][:], page[t][:].indirect(offsets[:]))
+
+        gates = [keep.tile([P, W], F32, name=f"gate_{i}") for i in range(3)]
+        fresh = [keep.tile([P, S], F32, name=f"fresh_{t}") for t in range(PACK)]
+        step = placed("step", [P, W], F32, 67)
+
+        def make_gate(i):
+            t, half = UNITS[i]
+            bank = banks[2 * (i % PACK)]
+
             def w4_slice(a):
                 first = a * N + t * P
                 return w4_codes[:, 2 * first : 2 * (first + P)].bitcast(FP4X4), w4_plane[:, first : first + P]
 
             second_product(bank, half, w4_slice)
-            gate[t, half] = into
-            nc.scalar.activation(into, bank[:], ACT.Sigmoid)
+            nc.scalar.activation(gates[i % len(gates)][:], bank[:], ACT.Sigmoid)
 
-        def make_step(t, half, bank, into):
-            cols = slice(t * P, (t + 1) * P)
-            second_product(bank, half, lambda a: (codes["w2", a, 0][:, cols].bitcast(FP8X4), planes["w2", a, 0][:, cols]))
-            step[t, half] = into
-            nc.vector.tensor_tensor(into, bank[:], gate[t, half], ALU.mult)
+        def copy_sum(i):
+            t, half = UNITS[i]
+            bank, cols = banks[2 * (i % PACK) + 1], slice(t * P, (t + 1) * P)
+            second_product(bank, half, lambda a: (w_codes["w2", a, 0][:, cols].bitcast(FP8X4), w_plane["w2", a, 0][:, cols]))
+            nc.scalar.copy(fresh[t][:, half * W : (half + 1) * W], bank[:])
 
-        def scatter(t, half):
-            nc.vector.tensor_tensor(listed(page[t][:], half), state[t, half], step[t, half], ALU.add)
-
-        def as_float32(rows):
-            return rows.rearrange("p t c -> p (t c)").bitcast(F32)
+        def finish(i, into=None):
+            t, half = UNITS[i]
+            lo, hi = half * W, (half + 1) * W
+            new = fresh[t][:, lo:hi]
+            nc.gpsimd.tensor_tensor(step[:], new, gates[i % len(gates)][:], ALU.mult)
+            nc.gpsimd.tensor_tensor(new if into is None else into, step[:], state[t][:, lo:hi], ALU.add)
+            if t < PACK - 1:
+                nc.vector.tensor_copy(listed(page[t][:], lo, hi), new if into is None else into)
+            elif half == 1:
+                nc.vector.tensor_copy(page[t][:].indirect(offsets[:]), fresh[t][:])
 
         gather_words(0, 0)
         gather_plane(0)
-        prepare_weight("w1", 0, 0, on_scalar, staging[0])
-        prepare_weight("w1", 1, 0, on_scalar, staging[1])
-        gather_words(1, 0)
-        hidden(0, 0)
-        prepare_weight("w1", 0, 1, on_vector, staging[2])
-        prepare_weight("w1", 1, 1, on_vector, staging[3])
-        hidden(0, 1)
-        quantise_hidden(0, 0, staging[0])
-        quantise_hidden(0, 1, staging[1])
-        prepare_weight("w2", 0, 0, on_vector, staging[2])
-        prepare_weight("w2", 1, 0, on_scalar, staging[3])
+        prepare_weight("w1", 0, 0, staging[0], P)
         gather_words(0, 1)
+        prepare_weight("w1", 1, 0, staging_once, 64)
+        w4_plane = placed("w4_plane", [P, PASSES * N], U8, 61)
+        nc.gpsimd.tensor_copy(
+            w4_plane[:].rearrange("p (a t m) -> p a t m", a=PASSES, t=PACK),
+            w4_plane_raw[:].bitcast(U8).rearrange("p (a m t) -> p a t m", a=PASSES, t=PACK),
+        )
         gather_plane(1)
+        gather_words(1, 0)
+        rows = {(0, 0): keep.tile([P, PACK, W], BF16, name="rows_0_0", align_bytes=64)}
+        hidden(0, 0, rows[0, 0])
+        prepare_weight("w1", 0, 1, staging[1], 0)
         gather_words(1, 1)
-
-        spent = raw["w2", 1, 0]
-        make_gate(0, 0, b_banks[0], spent[:, 2, :])
-        make_gate(1, 0, b_banks[1], spent[:, 3, :])
-        for t in range(PACK - 1):
-            gather_state(t, keep.tile([P, S], F32, name=f"state_{t}")[:])
-        make_step(0, 0, a_banks[0], step_ring[0][:])
-        make_step(1, 0, a_banks[1], step_ring[1][:])
-        h_rows[1, 0] = spent[:, 0:2, :].rearrange("p j c -> p (j c)").bitcast(BF16).rearrange("p (t c) -> p t c", t=PACK)
-        hidden(1, 0)
-        quantise_hidden(1, 0, staging[0])
-        make_gate(2, 0, b_banks[0], as_float32(h_rows[1, 0])[:, 0:W])
-        hidden(1, 1)
-        quantise_hidden(1, 1, staging[1])
-        last_state = as_float32(h_rows[1, 1])
-        gather_state(PACK - 1, last_state)
-        scatter(0, 0)
-        scatter(1, 0)
-        make_step(2, 0, a_banks[0], step_ring[2][:])
-        scatter(2, 0)
-
-        late = [(0, 1), (1, 1), (2, 1), (3, 0), (3, 1)]
-        last_steps = keep.tile([P, S], F32, name="last_steps")
-        late_b_banks = [b_banks[1], b_banks[0], h_banks[0], h_banks[1], h_banks[2]]
-        late_a_banks = [a_banks[1], h_banks[3], a_banks[0]]
-        for i, (t, half) in enumerate(late):
-            make_gate(t, half, late_b_banks[i], keep.tile([P, W], F32, name=f"gate_{t}_{half}")[:])
-            into = last_steps[:, half * W : (half + 1) * W] if t == PACK - 1 else step_ring[len(step) % len(step_ring)][:]
-            make_step(t, half, late_a_banks[i % len(late_a_banks)], into)
-            if t > 0 and half == 1:
-                scatter(t - 1, 1)
-        nc.vector.tensor_tensor(page[PACK - 1][:].indirect(offsets[:]), last_state, last_steps[:], ALU.add)
+        prepare_weight("w1", 1, 1, placed("staging_w1_last", [P, PACK * W], BF16, 48), 56)
+        woven = {(0, 0): placed("woven_0_0", [P, PACK * W], BF16, 48)}
+        weave_on_gpsimd(woven[0, 0], rows[0, 0])
+        gather_state(0)
+        rows[0, 1] = keep.tile([P, PACK, W], BF16, name="rows_0_1", align_bytes=64)
+        hidden(0, 1, rows[0, 1])
+        rows[1, 0] = placed("rows_1_0", [P, PACK, W], BF16, 24)
+        hidden(1, 0, rows[1, 0])
+        quantise_hidden(0, 0, woven[0, 0])
+        woven[0, 1] = staging[0]
+        weave_on_scalar(woven[0, 1], rows[0, 1])
+        prepare_weight("w2", 0, 0, staging[1], 0)
+        staging_last = placed("staging_w2_last", [P, PACK * W], BF16, 52)
+        round_weight("w2", 1, 0, staging_last, 0)
+        quantise_hidden(0, 1, woven[0, 1])
+        quantise_weight("w2", 1, 0, staging_last)
+        woven_late = placed("woven_late", [P, PASSES, PACK * W], BF16, 52)
+        woven[1, 0], woven[1, 1] = woven_late[:, 0, :], woven_late[:, 1, :]
+        weave_on_gpsimd(woven[1, 0], rows[1, 0])
+        gather_state(1)
+        rows[1, 1] = rows[0, 0]
+        hidden(1, 1, rows[1, 1])
+        for i in range(2):
+            make_gate(i)
+        copy_sum(0)
+        weave_on_scalar(woven[1, 1], rows[1, 1])
+        gather_state(2)
+        late_codes = placed("h_codes_late", [P, S], U32, 28)
+        late_plane = placed("h_plane_late", [P, S], U8, 24)
+        nc.vector.quantize_mx(out=late_codes[:].bitcast(FP8X4), scales=late_plane[:], in_=woven_late[:].rearrange("p b c -> p (b c)"))
+        for b in range(PASSES):
+            h_codes[1, b], h_plane[1, b] = late_codes[:, b * W : (b + 1) * W], late_plane[:, b * W : (b + 1) * W]
+        finish(0, placed("held", [P, W], F32, 52)[:])
+        gather_state(3)
+        copy_sum(1)
+        finish(1)
+        for i in range(2, len(UNITS)):
+            make_gate(i)
+            copy_sum(i)
+            finish(i)
         for t in range(PACK):
             nc.sync.dma_start(out_0.rearrange("(p t) m -> t p m", t=PACK)[t], page[t][:])
 
-        y_rows = [keep.tile([P, PACK, W], BF16, name=f"y_rows_{c}") for c in range(CHUNKS)]
-        y_woven = [
-            keep.tile([P, W, PACK], BF16, name=f"y_woven_{c}", tag=f"raw_w1_{c % 2}_{c // 2}", align_bytes=64)
-            for c in range(CHUNKS)
-        ]
+        y_woven = [placed(f"y_woven_{c}", [P, W, PACK], BF16, 4 * c) for c in range(CHUNKS)]
+        y_rows = [placed(f"y_rows_{c}", [P, PACK, W], BF16, 16 + 4 * c) for c in range(CHUNKS)]
         y_plane = keep.tile([P, T], U8, name="y_plane", align_bytes=64)
+        vector_chunks, scalar_chunks = (0, 1), (2, 3)
 
         def chunk_of_page(t, c):
             return page[t][:, c * W : (c + 1) * W]
 
-        def weave(c, first, last, copy):
+        y_tail = [placed(f"y_tail_{c}", [P, 2, W], BF16, 66 + 2 * c) for c in vector_chunks]
+
+        def weave_result(c, first, last, copy):
+            rows = y_tail[c][:] if first == 2 else y_rows[c][:, first:last, :]
             copy(
                 y_woven[c][:, :, first:last].rearrange("p (c i) t -> p c t i", i=RUN),
-                y_rows[c][:, first:last, :].rearrange("p t (c i) -> p c t i", i=RUN),
+                rows.rearrange("p t (c i) -> p c t i", i=RUN),
             )
 
         for t in range(PACK - 1):
-            for c in range(CHUNKS):
-                nc.scalar.copy(y_rows[c][:, t, :], chunk_of_page(t, c))
+            for c in scalar_chunks + vector_chunks if t == 2 else range(CHUNKS):
+                if t == 2 and c in vector_chunks:
+                    nc.gpsimd.tensor_copy(y_tail[c][:, 0, :], chunk_of_page(t, c))
+                else:
+                    on_scalar(y_rows[c][:, t, :], chunk_of_page(t, c))
+                if t == 2 and c in scalar_chunks:
+                    weave_result(c, 0, 3, on_scalar)
             if t == 1:
-                for c in VECTOR_CHUNKS:
-                    weave(c, 0, 2, on_scalar)
-        for c in SCALAR_CHUNKS:
-            weave(c, 0, 3, on_scalar)
-        for c in SCALAR_CHUNKS:
+                for c in vector_chunks:
+                    weave_result(c, 0, 2, on_scalar)
+        for c in scalar_chunks:
             nc.scalar.copy(y_woven[c][:, :, 3], chunk_of_page(3, c))
-        for c in VECTOR_CHUNKS:
-            nc.vector.tensor_copy(y_rows[c][:, 3, :], chunk_of_page(3, c))
-        for c in VECTOR_CHUNKS:
-            weave(c, 2, 4, on_vector)
+        for c in vector_chunks:
+            nc.vector.tensor_copy(y_tail[c][:, 1, :], chunk_of_page(3, c))
+        for c in vector_chunks:
+            weave_result(c, 2, 4, on_vector)
 
         out_words = out_1[0].rearrange("p m i -> p (m i)").bitcast(I32)
         for c in range(CHUNKS):

@@ -221,12 +221,14 @@ def tile_list_stroke_correction_kernel(
             t, half = UNITS[i]
             lo, hi = half * W, (half + 1) * W
             new = fresh[t][:, lo:hi]
-            nc.gpsimd.tensor_tensor(step[:], new, gates[i % len(gates)][:], ALU.mult)
-            nc.gpsimd.tensor_tensor(new if into is None else into, step[:], state[t][:, lo:hi], ALU.add)
             if t < PACK - 1:
+                nc.gpsimd.tensor_tensor(step[:], new, gates[i % len(gates)][:], ALU.mult)
+                nc.gpsimd.tensor_tensor(new if into is None else into, step[:], state[t][:, lo:hi], ALU.add)
                 nc.vector.tensor_copy(listed(page[t][:], lo, hi), new if into is None else into)
-            elif half == 1:
-                nc.vector.tensor_copy(page[t][:].indirect(offsets[:]), fresh[t][:])
+            else:
+                nc.gpsimd.tensor_tensor(last_steps[:, lo:hi], new, gates[i % len(gates)][:], ALU.mult)
+                if half == 1:
+                    nc.vector.tensor_tensor(page[t][:].indirect(offsets[:]), state[t][:], last_steps[:], ALU.add)
 
         gather_words(0, 0)
         gather_plane(0)
@@ -281,6 +283,8 @@ def tile_list_stroke_correction_kernel(
         copy_sum(1)
         finish(1)
         for i in range(2, len(UNITS)):
+            if UNITS[i] == (PACK - 1, 0):
+                last_steps = placed("last_steps", [P, S], F32, 67)
             make_gate(i)
             copy_sum(i)
             finish(i)
@@ -295,7 +299,7 @@ def tile_list_stroke_correction_kernel(
         def chunk_of_page(t, c):
             return page[t][:, c * W : (c + 1) * W]
 
-        y_tail = [placed(f"y_tail_{c}", [P, 2, W], BF16, 66 + 2 * c) for c in vector_chunks]
+        y_tail = [placed(f"y_tail_{c}", [P, 2, W], BF16, 72 + 2 * c) for c in vector_chunks]
 
         def weave_result(c, first, last, copy):
             rows = y_tail[c][:] if first == 2 else y_rows[c][:, first:last, :]
@@ -307,7 +311,7 @@ def tile_list_stroke_correction_kernel(
         for t in range(PACK - 1):
             for c in scalar_chunks + vector_chunks if t == 2 else range(CHUNKS):
                 if t == 2 and c in vector_chunks:
-                    nc.gpsimd.tensor_copy(y_tail[c][:, 0, :], chunk_of_page(t, c))
+                    on_scalar(y_tail[c][:, 0, :], chunk_of_page(t, c))
                 else:
                     on_scalar(y_rows[c][:, t, :], chunk_of_page(t, c))
                 if t == 2 and c in scalar_chunks:

@@ -168,7 +168,9 @@ def tile_list_stroke_correction_kernel(
             )
 
         def weave_on_gpsimd(woven, rows):
-            nc.gpsimd.tensor_copy(woven[:].rearrange("p (c t) -> p c t", t=PACK), rows[:].rearrange("p t c -> p c t"))
+            nc.gpsimd.tensor_scalar(
+                woven[:].rearrange("p (c t) -> p c t", t=PACK), rows[:].rearrange("p t c -> p c t"), 1.0, 0.0, ALU.mult, ALU.add
+            )
 
         h_codes, h_plane = {}, {}
 

from contextlib import ExitStack

import concourse.mybir as mybir

K, H, N, T, S = 1024, 1024, 512, 2048, 1024
FLOPS = 2 * K * H * S + 2 * 2 * H * N * S

F32 = mybir.dt.float32
BF16 = mybir.dt.bfloat16
I32 = mybir.dt.int32
U32 = mybir.dt.uint32
U16 = mybir.dt.uint16
U8 = mybir.dt.uint8
FP8X4 = mybir.dt.float8_e4m3fn_x4
FP4X4 = mybir.dt.float4_e2m1fn_x4
ACT = mybir.ActivationFunctionType
ALU = mybir.AluOpType

P = 128
PACK = 4
W = P * PACK
PASSES = 2
QUADS = 4
PER_COLUMN = 16
CHUNKS = T // W
RUN = 4
KIB = 1024
UNITS = ((0, 0), (1, 0), (0, 1), (1, 1), (2, 0), (2, 1), (3, 0), (3, 1))


def tile_list_stroke_correction_kernel(
    tc, tab_words, tab_scales, offs, gT, w1, b1, w2, w4_words, w4_scales, out_0, out_1, out_2
):
    nc = tc.nc
    on_scalar, on_vector = nc.scalar.copy, nc.vector.tensor_copy

    with ExitStack() as ctx:
        keep = ctx.enter_context(tc.tile_pool(name="keep", bufs=1))
        shared = ctx.enter_context(tc.tile_pool(name="shared", bufs=1))
        psum = ctx.enter_context(tc.psum_pool(name="psum", bufs=1))

        def placed(name, shape, dtype, kib):
            return shared.tile(shape, dtype, name=name, align_bytes=64, offset=int(kib * KIB))

        offsets = keep.tile([P, S // PER_COLUMN], U16, name="offsets")
        nc.sync.dma_start(offsets[:], offs)

        def listed(window, lo, hi):
            return window.indirect(offsets[:, lo // PER_COLUMN : hi // PER_COLUMN])

        tab_plane = keep.tile([P, T // 4], I32, name="tab_plane", align_bytes=64)
        w4_plane_raw = keep.tile([P, PASSES * N // 4], I32, name="w4_plane_raw", align_bytes=64)
        nc.vector.memset(tab_plane[:], 0)
        nc.vector.memset(w4_plane_raw[:], 0)

        bias = keep.tile([P, PASSES, PACK], F32, name="bias")
        nc.scalar.dma_start(bias[:], b1.rearrange("(b p t) -> p b t", b=PASSES, t=PACK))
        w4_raw = keep.tile([P, PASSES * 2 * N // 4], I32, name="w4_raw", align_bytes=64)
        nc.sync.dma_start(
            w4_raw[:].rearrange("p (a c) -> p a c", a=PASSES), w4_words.bitcast(I32).rearrange("a p c -> p a c")
        )
        for q in range(QUADS):
            nc.scalar.dma_start(tab_plane[32 * q : 32 * q + 8, :], tab_scales[:, 4 * q : 4 * q + 4, :].bitcast(I32))
        for q in range(QUADS):
            nc.scalar.dma_start(
                w4_plane_raw[32 * q : 32 * q + 4, :].rearrange("p (a c) -> p a c", a=PASSES),
                w4_scales[:, 4 * q : 4 * q + 4, :].bitcast(I32).rearrange("a r c -> r a c"),
            )

        raw, tab_raw, page = {}, {}, {}
        raw_place = {("w1", 0, 0): 0, ("w1", 1, 0): 8, ("w1", 0, 1): 16, ("w1", 1, 1): 24, ("w2", 0, 0): 32, ("w2", 1, 0): 40}

        def load_weight(name, src, a, b):
            raw[name, a, b] = placed(f"raw_{name}_{a}_{b}", [P, PACK, W], F32, raw_place[name, a, b])
            rows = src[a * W : (a + 1) * W, b * W : (b + 1) * W]
            nc.sync.dma_start(raw[name, a, b][:], rows.rearrange("(p j) c -> p j c", j=PACK))

        def load_table(a):
            tab_raw[a] = keep.tile([P, T], I32, name=f"tab_raw_{a}")
            nc.sync.dma_start(tab_raw[a][:], tab_words[a].rearrange("p n i -> p (n i)").bitcast(I32))

        def load_page(t):
            page[t] = keep.tile([P, T], F32, name=f"page_{t}")
            nc.sync.dma_start(page[t][:], gT.rearrange("(p t) m -> t p m", t=PACK)[t])

        load_table(0)
        load_weight("w1", w1, 0, 0)
        load_weight("w1", w1, 1, 0)
        load_table(1)
        load_weight("w1", w1, 0, 1)
        load_weight("w1", w1, 1, 1)
        load_page(0)
        load_weight("w2", w2, 0, 0)
        load_weight("w2", w2, 1, 0)
        for t in range(1, PACK):
            load_page(t)

        warm_out = keep.tile([P, 1], F32, name="warm_out")
        nc.scalar.activation(warm_out[:], bias[:, 0, 0:1], ACT.Sigmoid)

        staging = [keep.tile([P, PACK * W], BF16, name=f"staging_{i}", align_bytes=64) for i in range(2)]
        staging_once = placed("staging_once", [P, PACK * W], BF16, 61)
        w_codes, w_plane = {}, {}

        def round_weight(name, a, b, woven, on_scalar_to):
            key = name, a, b
            out = woven[:].rearrange("p (t m j) -> p m j t", t=PACK, j=PACK)
            src = raw[key][:].rearrange("p j (m t) -> p m j t", t=PACK)
            if on_scalar_to > 0:
                on_scalar(out[:, :on_scalar_to], src[:, :on_scalar_to])
            if on_scalar_to < P:
                on_vector(out[:, on_scalar_to:], src[:, on_scalar_to:])

        def prepare_weight(name, a, b, woven, on_scalar_to):
            round_weight(name, a, b, woven, on_scalar_to)
            quantise_weight(name, a, b, woven)

        def quantise_weight(name, a, b, woven):
            key = name, a, b
            if name == "w2":
                w_codes[key] = placed(f"codes_w2_{a}", [P, W], U32, 16 + 4 * a)
            else:
                w_codes[key] = keep.tile([P, W], U32, name=f"codes_{name}_{a}_{b}", align_bytes=64)
            w_plane[key] = keep.tile([P, W], U8, name=f"plane_{name}_{a}_{b}", align_bytes=64)
            nc.vector.quantize_mx(out=w_codes[key][:].bitcast(FP8X4), scales=w_plane[key][:], in_=woven[:])

        w4_codes = keep.tile([P, PASSES * 2 * N], U8, name="w4_codes", align_bytes=64)
        nc.vector.tensor_copy(
            w4_codes[:].bitcast(U16).rearrange("p (a t m) -> p a t m", a=PASSES, t=PACK),
            w4_raw[:].bitcast(U16).rearrange("p (a m t) -> p a t m", a=PASSES, t=PACK),
        )

        v_codes = [keep.tile([P, S], U32, name=f"v_codes_{a}", align_bytes=64) for a in range(PASSES)]
        v_plane = keep.tile([P, S], U8, name="v_plane", align_bytes=64)

        def gather_words(a, half):
            lo, hi = half * W, (half + 1) * W
            nc.vector.tensor_copy(v_codes[a][:, lo:hi], listed(tab_raw[a][:].bitcast(U32), lo, hi))

        def gather_plane(half):
            lo, hi = half * W, (half + 1) * W
            nc.vector.tensor_copy(v_plane[:, lo:hi], listed(tab_plane[:].bitcast(U8), lo, hi))

        banks = [psum.tile([P, W], F32, name=f"bank_{i}") for i in range(2 * PACK)]

        def hidden(half, b, rows):
            sums = banks[half * PACK : (half + 1) * PACK]
            entries = slice(half * W, (half + 1) * W)
            for a in range(PASSES):
                for t in range(PACK):
                    cols = slice(t * P, (t + 1) * P)
                    nc.tensor.matmul_mx(
                        out=sums[t][:],
                        lhsT=w_codes["w1", a, b][:, cols].bitcast(FP8X4),
                        lhsT_scale=w_plane["w1", a, b][:, cols],
                        rhs=v_codes[a][:, entries].bitcast(FP8X4),
                        rhs_scale=v_plane[4 * a : P, entries],
                        start=(a == 0),
                        stop=(a == PASSES - 1),
                    )
            for t in range(PACK):
                nc.scalar.activation(rows[:, t, :], sums[t][:], ACT.Relu, bias=bias[:, b, t : t + 1])

        def weave_on_scalar(woven, rows):
            nc.scalar.copy(
                woven[:].rearrange("p (c i t) -> p c t i", i=RUN, t=PACK),
                rows[:].rearrange("p t (c i) -> p c t i", i=RUN),
            )

        def weave_on_gpsimd(woven, rows):
            nc.gpsimd.tensor_scalar(
                woven[:].rearrange("p (c t) -> p c t", t=PACK), rows[:].rearrange("p t c -> p c t"), 1.0, 0.0, ALU.mult, ALU.add
            )

        h_codes, h_plane = {}, {}

        def quantise_hidden(half, b, woven):
            h_codes[half, b] = keep.tile([P, W], U32, name=f"h_codes_{half}_{b}", align_bytes=64)
            h_plane[half, b] = keep.tile([P, W], U8, name=f"h_plane_{half}_{b}", align_bytes=64)
            nc.vector.quantize_mx(out=h_codes[half, b][:].bitcast(FP8X4), scales=h_plane[half, b][:], in_=woven[:])

        def second_product(bank, half, weight):
            for a in range(PASSES):
                lhsT, lhsT_scale = weight(a)
                nc.tensor.matmul_mx(
                    out=bank[:],
                    lhsT=lhsT,
                    lhsT_scale=lhsT_scale,
                    rhs=h_codes[half, a][:].bitcast(FP8X4),
                    rhs_scale=h_plane[half, a][:],
                    start=(a == 0),
                    stop=(a == PASSES - 1),
                )

        state = {}

        def gather_state(t):
            state[t] = keep.tile([P, S], F32, name=f"state_{t}")
            nc.vector.tensor_copy(state[t][:], page[t][:].indirect(offsets[:]))

        gates = [keep.tile([P, W], F32, name=f"gate_{i}") for i in range(3)]
        fresh = [keep.tile([P, S], F32, name=f"fresh_{t}") for t in range(PACK)]
        step = placed("step", [P, W], F32, 67)

        def make_gate(i):
            t, half = UNITS[i]
            bank = banks[2 * (i % PACK)]

            def w4_slice(a):
                first = a * N + t * P
                return w4_codes[:, 2 * first : 2 * (first + P)].bitcast(FP4X4), w4_plane[:, first : first + P]

            second_product(bank, half, w4_slice)
            nc.scalar.activation(gates[i % len(gates)][:], bank[:], ACT.Sigmoid)

        def copy_sum(i):
            t, half = UNITS[i]
            bank, cols = banks[2 * (i % PACK) + 1], slice(t * P, (t + 1) * P)
            second_product(bank, half, lambda a: (w_codes["w2", a, 0][:, cols].bitcast(FP8X4), w_plane["w2", a, 0][:, cols]))
            nc.scalar.copy(fresh[t][:, half * W : (half + 1) * W], bank[:])

        def finish(i, into=None):
            t, half = UNITS[i]
            lo, hi = half * W, (half + 1) * W
            new = fresh[t][:, lo:hi]
            if t < PACK - 1:
                nc.gpsimd.tensor_tensor(step[:], new, gates[i % len(gates)][:], ALU.mult)
                nc.gpsimd.tensor_tensor(new if into is None else into, step[:], state[t][:, lo:hi], ALU.add)
                nc.vector.tensor_copy(listed(page[t][:], lo, hi), new if into is None else into)
            else:
                nc.gpsimd.tensor_tensor(last_steps[:, lo:hi], new, gates[i % len(gates)][:], ALU.mult)
                if half == 1:
                    nc.vector.tensor_tensor(page[t][:].indirect(offsets[:]), state[t][:], last_steps[:], ALU.add)

        gather_words(0, 0)
        gather_plane(0)
        prepare_weight("w1", 0, 0, staging[0], P)
        gather_words(0, 1)
        prepare_weight("w1", 1, 0, staging_once, 64)
        w4_plane = placed("w4_plane", [P, PASSES * N], U8, 61)
        nc.gpsimd.tensor_copy(
            w4_plane[:].rearrange("p (a t m) -> p a t m", a=PASSES, t=PACK),
            w4_plane_raw[:].bitcast(U8).rearrange("p (a m t) -> p a t m", a=PASSES, t=PACK),
        )
        gather_plane(1)
        gather_words(1, 0)
        rows = {(0, 0): keep.tile([P, PACK, W], BF16, name="rows_0_0", align_bytes=64)}
        hidden(0, 0, rows[0, 0])
        prepare_weight("w1", 0, 1, staging[1], 0)
        gather_words(1, 1)
        prepare_weight("w1", 1, 1, placed("staging_w1_last", [P, PACK * W], BF16, 48), 56)
        woven = {(0, 0): placed("woven_0_0", [P, PACK * W], BF16, 48)}
        weave_on_gpsimd(woven[0, 0], rows[0, 0])
        gather_state(0)
        rows[0, 1] = keep.tile([P, PACK, W], BF16, name="rows_0_1", align_bytes=64)
        hidden(0, 1, rows[0, 1])
        rows[1, 0] = placed("rows_1_0", [P, PACK, W], BF16, 24)
        hidden(1, 0, rows[1, 0])
        quantise_hidden(0, 0, woven[0, 0])
        woven[0, 1] = staging[0]
        weave_on_scalar(woven[0, 1], rows[0, 1])
        prepare_weight("w2", 0, 0, staging[1], 0)
        staging_last = placed("staging_w2_last", [P, PACK * W], BF16, 52)
        round_weight("w2", 1, 0, staging_last, 0)
        quantise_hidden(0, 1, woven[0, 1])
        quantise_weight("w2", 1, 0, staging_last)
        woven_late = placed("woven_late", [P, PASSES, PACK * W], BF16, 52)
        woven[1, 0], woven[1, 1] = woven_late[:, 0, :], woven_late[:, 1, :]
        weave_on_gpsimd(woven[1, 0], rows[1, 0])
        gather_state(1)
        rows[1, 1] = rows[0, 0]
        hidden(1, 1, rows[1, 1])
        for i in range(2):
            make_gate(i)
        copy_sum(0)
        weave_on_scalar(woven[1, 1], rows[1, 1])
        gather_state(2)
        late_codes = placed("h_codes_late", [P, S], U32, 28)
        late_plane = placed("h_plane_late", [P, S], U8, 24)
        nc.vector.quantize_mx(out=late_codes[:].bitcast(FP8X4), scales=late_plane[:], in_=woven_late[:].rearrange("p b c -> p (b c)"))
        for b in range(PASSES):
            h_codes[1, b], h_plane[1, b] = late_codes[:, b * W : (b + 1) * W], late_plane[:, b * W : (b + 1) * W]
        finish(0, placed("held", [P, W], F32, 52)[:])
        gather_state(3)
        copy_sum(1)
        finish(1)
        for i in range(2, len(UNITS)):
            if UNITS[i] == (PACK - 1, 0):
                last_steps = placed("last_steps", [P, S], F32, 67)
            make_gate(i)
            copy_sum(i)
            finish(i)
        for t in range(PACK):
            nc.sync.dma_start(out_0.rearrange("(p t) m -> t p m", t=PACK)[t], page[t][:])

        y_woven = [placed(f"y_woven_{c}", [P, W, PACK], BF16, 4 * c) for c in range(CHUNKS)]
        y_rows = [placed(f"y_rows_{c}", [P, PACK, W], BF16, 16 + 4 * c) for c in range(CHUNKS)]
        y_plane = keep.tile([P, T], U8, name="y_plane", align_bytes=64)
        vector_chunks, scalar_chunks = (0, 1), (2, 3)

        def chunk_of_page(t, c):
            return page[t][:, c * W : (c + 1) * W]

        y_tail = [placed(f"y_tail_{c}", [P, 2, W], BF16, 72 + 2 * c) for c in vector_chunks]

        def weave_result(c, first, last, copy):
            rows = y_tail[c][:] if first == 2 else y_rows[c][:, first:last, :]
            copy(
                y_woven[c][:, :, first:last].rearrange("p (c i) t -> p c t i", i=RUN),
                rows.rearrange("p t (c i) -> p c t i", i=RUN),
            )

        for t in range(PACK - 1):
            for c in scalar_chunks + vector_chunks if t == 2 else range(CHUNKS):
                if t == 2 and c in vector_chunks:
                    on_scalar(y_tail[c][:, 0, :], chunk_of_page(t, c))
                else:
                    on_scalar(y_rows[c][:, t, :], chunk_of_page(t, c))
                if t == 2 and c in scalar_chunks:
                    weave_result(c, 0, 3, on_scalar)
            if t == 1:
                for c in vector_chunks:
                    weave_result(c, 0, 2, on_scalar)
        for c in scalar_chunks:
            nc.scalar.copy(y_woven[c][:, :, 3], chunk_of_page(3, c))
        for c in vector_chunks:
            nc.vector.tensor_copy(y_tail[c][:, 1, :], chunk_of_page(3, c))
        for c in vector_chunks:
            weave_result(c, 2, 4, on_vector)

        out_words = out_1[0].rearrange("p m i -> p (m i)").bitcast(I32)
        for c in range(CHUNKS):
            cols = slice(c * W, (c + 1) * W)
            y_codes = keep.tile([P, W], I32, name=f"y_codes_{c}", align_bytes=64)
            nc.vector.quantize_mx(
                out=y_codes[:].bitcast(FP8X4), scales=y_plane[:, cols], in_=y_woven[c][:].rearrange("p m t -> p (m t)")
            )
            nc.sync.dma_start(out_words[:, cols], y_codes[:])
        for q in range(QUADS):
            queue = nc.scalar if q % 2 else nc.sync
            queue.dma_start(out_2[0, 4 * q : 4 * q + 4, :].bitcast(I32), y_plane[32 * q : 32 * q + 4, :].bitcast(I32))
